import numpy as np
import ml_dtypes


def mxq(x, axis, fmt="e4m3"):
    dtype, down = {"e4m3": (ml_dtypes.float8_e4m3fn, 7), "e5m2": (ml_dtypes.float8_e5m2, 14)}[fmt]
    v = np.moveaxis(np.asarray(x, np.float32).astype(ml_dtypes.bfloat16).astype(np.float64), axis, -1)
    blocks = v.reshape(v.shape[:-1] + (-1, 32))
    amax = np.abs(blocks).max(-1, keepdims=True)
    byte = np.maximum(np.where(amax > 0, np.frexp(amax)[1] - 1 + 127, 0) - down, 1)
    scale = np.exp2(byte - 127.0)
    codes = (blocks / scale).astype(np.float32).astype(dtype).astype(np.float64)
    return np.moveaxis((codes * scale).reshape(v.shape), -1, axis)


WIDE = False


def mx_kscale(k):
    if not WIDE:
        return np.ones(k)
    levels = np.array([10, -10, 5, -5, 0])
    if k % 512:
        return np.exp2(np.random.permutation(np.resize(levels, k // 32))).repeat(32)
    a = np.empty((k // 512, 16))
    for p in range(k // 512):
        a[p, :8] = np.random.permutation(np.resize(levels, 8))
        for g in range(8):
            far = levels[np.abs(levels - a[p, g]) >= 10]
            a[p, g + 8] = far[np.random.randint(len(far))]
    return np.exp2(a.ravel()).repeat(32)


BF16 = ml_dtypes.bfloat16


def bf(x):
    return np.asarray(x, np.float32).astype(BF16)


def f64(x):
    return np.asarray(x).astype(np.float64)

def planes(Y):
    n, m = Y.shape
    b = f64(bf(Y)).reshape(n // 32, 32, m)
    amax = np.abs(b).max(1)
    byte = np.clip(np.where(amax > 0, np.frexp(amax)[1] - 1 + 127 - 7, 1), 1, 254)
    codes = (b * np.exp2(127.0 - byte)[:, None, :]).reshape(n, m).astype(np.float32).astype(ml_dtypes.float8_e4m3fn).view(np.uint8)
    words = codes.reshape(n // 512, 128, 4, m).transpose(0, 1, 3, 2)
    return np.ascontiguousarray(words), np.ascontiguousarray(byte.astype(np.uint8).reshape(n // 512, 16, m))


N, K, P, Q = 1024, 1024, 1024, 1024


def root(size):
    return np.sqrt(size)


def setup_inputs():
    u, t = mx_kscale(N), mx_kscale(K)
    r = 0.5 + np.random.random_sample((N, 1))
    return {
        "a": bf(np.random.standard_normal((N, P)) / u[:, None]),
        "y": bf(np.random.standard_normal((N, Q)) / u[:, None]),
        "phi": bf(np.random.standard_normal((N, K)) * r * u[:, None] * t[None, :]),
        "omega": bf((0.7 + 0.2 * np.random.standard_normal(K)) / (t * t)),
    }


def core(a, y, phi, omega):
    a, y, phi, omega = f64(a), f64(y), f64(phi), f64(omega)
    n, k = phi.shape
    aq = mxq(a, 0, "e4m3")
    yq = mxq(y, 0, "e4m3")
    pq = mxq(phi, 0, "e4m3")
    g1 = (aq.T @ pq) / root(n)
    g2 = (pq.T @ yq) / root(n)
    full = mxq(g1 * omega[None, :], 1, "e4m3") @ mxq(g2, 0, "e4m3")
    h = np.sum(omega[None, :] * np.square(phi), axis=1) / n
    diag = mxq(a * h[:, None], 0, "e4m3").T @ yq
    return (full - diag) / root(k)


def reference(a, y, phi, omega):
    R_out = core(a, y, phi, omega)
    words, scales = planes(R_out)
    return R_out, words, scales

@@ -1,0 +1,228 @@
+from contextlib import ExitStack
+
+import concourse.mybir as mybir
+
+N = 1024
+FLOPS = 4 * 2 * N * N * N
+
+F32 = mybir.dt.float32
+BF16 = mybir.dt.bfloat16
+U32 = mybir.dt.uint32
+I32 = mybir.dt.int32
+U8 = mybir.dt.uint8
+FP8X4 = mybir.dt.float8_e4m3fn_x4
+MULT = mybir.AluOpType.mult
+COPY = mybir.ActivationFunctionType.Copy
+SQUARE = mybir.ActivationFunctionType.Square
+
+P = 128
+PACK = 4
+HALF = 512
+ROOT = 1.0 / 32.0
+GB = 3
+LOADS = [('phi', 0, 0), ('y', 0, 0), ('phi', 1, 0), ('y', 1, 0), ('phi', 0, 1), ('phi', 1, 1), ('a', 0, 0), ('a', 1, 0), ('y', 0, 1), ('y', 1, 1), ('a', 0, 1), ('a', 1, 1)]
+ON_SCALAR = [('y', 0, 0), ('y', 0, 1), ('y', 1, 0), ('y', 1, 1), ('a', 0, 1), ('a', 1, 1), ('ah', 0, 1), ('ah', 1, 1)]
+ORDER = [("omb", 1), ("omb", 0), ("ob", 1), ("ob", 0), ("il_phi", 0, 0), ("sq", 0, 0), ("Q_phi", 0, 0), ("il_y", 0, 0), ("il_phi", 1, 0), ("Q_phi", 1, 0), ("il_y", 1, 0), ("il_phi", 0, 1), ("Q_y", 0, 0), ("il_phi", 1, 1), ("sq", 0, 1), ("Q_y", 1, 0), ("il_a", 1, 0), ("my", 0, 0, 0), ("sq", 1, 1), ("my", 0, 0, 1), ("my", 0, 0, 2), ("hs", 0, 3), ("my", 0, 0, 3), ("Q_phi", 1, 1), ("ey", 0, 0, 0), ("hs", 0, 2), ("il_a", 0, 1), ("Q_a", 1, 0), ("il_a", 0, 0), ("il_a", 1, 1), ("hs", 0, 0), ("Q_a", 0, 0), ("hs", 0, 1), ("ma", 0, 0, 0), ("ey", 0, 0, 1), ("ma", 0, 0, 1), ("ey", 0, 0, 2), ("Q_a", 1, 1), ("ma", 0, 0, 2), ("ey", 0, 0, 3), ("wt_", 0, 1), ("ma", 0, 0, 3), ("il_y", 1, 1), ("Qgy", 0, 0), ("Q_phi", 0, 1), ("wt_", 0, 0), ("my", 1, 0, 0), ("Q_a", 0, 1), ("my", 1, 0, 1), ("ey", 1, 0, 0), ("ea", 0, 0, 0), ("ma", 0, 1, 0), ("ey", 1, 0, 1), ("Q_y", 1, 1), ("ma", 0, 1, 1), ("il_y", 0, 1), ("ea", 0, 1, 0), ("ma", 0, 1, 2), ("ea", 0, 1, 1), ("ma", 0, 1, 3), ("ea", 0, 1, 2), ("ma", 1, 1, 0), ("ea", 0, 1, 3), ("ma", 1, 1, 1), ("ea", 1, 1, 0), ("sq", 1, 0), ("ma", 1, 1, 2), ("Q_y", 0, 1), ("ma", 1, 1, 3), ("ea", 1, 1, 1), ("my", 0, 1, 0), ("ea", 1, 1, 2), ("ea", 1, 1, 3), ("my", 0, 1, 1), ("il_ah", 0, 1), ("hs", 1, 2), ("my", 0, 1, 2), ("my", 0, 1, 3), ("hs", 1, 3), ("my", 1, 0, 2), ("ey", 0, 1, 0), ("hs", 1, 1), ("ey", 0, 1, 1), ("my", 1, 0, 3), ("ey", 0, 1, 2), ("my", 1, 1, 0), ("Qga", 1, 1), ("ey", 0, 1, 3), ("my", 1, 1, 1), ("hs", 1, 0), ("ey", 1, 1, 0), ("my", 1, 1, 2), ("ey", 1, 1, 1), ("my", 1, 1, 3), ("Qgy", 0, 1), ("ey", 1, 1, 2), ("ma", 1, 0, 0), ("wt_", 1, 1), ("ey", 1, 1, 3), ("ma", 1, 0, 1), ("Qga", 0, 1), ("ey", 1, 0, 2), ("ma", 1, 0, 2), ("Qgy", 1, 1), ("il_ah", 1, 1), ("ma", 1, 0, 3), ("ea", 0, 0, 1), ("ea", 0, 0, 2), ("f", 1, 1, 0), ("f", 1, 1, 1), ("ea", 0, 0, 3), ("f", 1, 1, 2), ("Q_ah", 0, 1), ("ey", 1, 0, 3), ("Q_ah", 1, 1), ("f", 1, 1, 3), ("Qgy", 1, 0), ("d", 1, 1, 0), ("Qga", 0, 0), ("d", 1, 1, 1), ("v", 1, 1, 0), ("ea", 1, 0, 0), ("d", 1, 1, 2), ("v", 1, 1, 1), ("ea", 1, 0, 1), ("d", 1, 1, 3), ("v", 1, 1, 2), ("ea", 1, 0, 2), ("f", 1, 0, 0), ("v", 1, 1, 3), ("ea", 1, 0, 3), ("f", 1, 0, 1), ("oi", 1, 1), ("f", 1, 0, 2), ("f", 1, 0, 3), ("d", 1, 0, 0), ("Qga", 1, 0), ("d", 1, 0, 1), ("oq", 1, 1), ("v", 1, 0, 0), ("f", 0, 1, 0), ("v", 1, 0, 1), ("wt_", 1, 0), ("f", 0, 1, 1), ("il_ah", 0, 0), ("f", 0, 1, 2), ("f", 0, 1, 3), ("il_ah", 1, 0), ("d", 1, 0, 2), ("d", 1, 0, 3), ("v", 1, 0, 2), ("f", 0, 0, 0), ("v", 1, 0, 3), ("Q_ah", 0, 0), ("f", 0, 0, 1), ("Q_ah", 1, 0), ("f", 0, 0, 2), ("oi", 1, 0), ("d", 0, 1, 0), ("d", 0, 1, 1), ("v", 0, 1, 0), ("oq", 1, 0), ("d", 0, 1, 2), ("v", 0, 1, 1), ("d", 0, 1, 3), ("v", 0, 1, 2), ("f", 0, 0, 3), ("v", 0, 1, 3), ("d", 0, 0, 0), ("oi", 0, 1), ("d", 0, 0, 1), ("v", 0, 0, 0), ("d", 0, 0, 2), ("v", 0, 0, 1), ("d", 0, 0, 3), ("oq", 0, 1), ("v", 0, 0, 2), ("v", 0, 0, 3), ("oi", 0, 0), ("oq", 0, 0)]
+
+
+def tile_secondorderinfluenceustatisticmatrix_x1_kernel(tc, a, y, phi, omega, out_0, out_1, out_2):
+    nc = tc.nc
+    with ExitStack() as ctx:
+        keep = ctx.enter_context(tc.tile_pool(name="keep", bufs=1))
+        work = ctx.enter_context(tc.tile_pool(name="work", bufs=3))
+        psum = ctx.enter_context(tc.psum_pool(name="psum", bufs=4))
+        ctx.enter_context(tc.manual_schedule())
+
+        def keep_tile(shape, dtype, name):
+            return keep.tile(shape, dtype, name=name, align_bytes=64)
+
+        raw = {}
+        codes = {}
+        scales = {}
+        group = {}
+
+        def load(key, src, g):
+            c = key[2]
+            t = keep_tile([P, PACK, HALF], BF16, "raw_%s_%d_%d" % key)
+            rows = src[g * HALF:(g + 1) * HALF, c * HALF:(c + 1) * HALF]
+            nc.sync.dma_start(out=t[:], in_=rows.rearrange("(p j) w -> p j w", j=PACK))
+            raw[key] = t
+
+        def permuted(t):
+            return t[:].rearrange("p j (m t) -> p t m j", t=PACK)
+
+        def interleave(engine_copy, key, natural):
+            t = work.tile([P, HALF * PACK], BF16, name="grp", tag="grp", bufs=6, align_bytes=64)
+            if natural:
+                engine_copy(out=t[:].rearrange("p (c j) -> p c j", j=PACK), in_=raw[key][:].rearrange("p j c -> p c j"))
+            else:
+                engine_copy(out=t[:].rearrange("p (t m j) -> p t m j", t=PACK, j=PACK), in_=permuted(raw[key]))
+            group[key] = t
+
+        def quantize(key, src=None):
+            q = keep_tile([P, HALF], U32, "codes_%s_%d_%d" % key)
+            s = keep_tile([P, HALF], U8, "scales_%s_%d_%d" % key)
+            nc.vector.quantize_mx(out=q[:].bitcast(FP8X4), scales=s[:], in_=(group[key] if src is None else src)[:])
+            codes[key] = q
+            scales[key] = s
+
+        omega_row = keep_tile([P, N], BF16, "omega_row")
+        ones = keep_tile([P, P], BF16, "ones")
+        omega_b = keep_tile([P, N], BF16, "omega_b")
+        omega_c = keep_tile([P, 2, PACK], BF16, "omega_c")
+        omega_s = keep_tile([P, 2, PACK], F32, "omega_s")
+        hneg = keep_tile([P, 2, PACK], F32, "hneg")
+        sq = [keep_tile([P, PACK, N], F32, "sq%d" % g) for g in range(2)]
+
+        def bank():
+            return psum.tile([P, HALF], F32, name="bank", tag="bank", bufs=8)
+
+        banks = {}
+        outf = {}
+        og = {}
+        V = nc.vector.tensor_copy
+        S = nc.scalar.copy
+
+        nc.vector.memset(omega_row[:], 0.0)
+        nc.vector.memset(ones[:], 1.0)
+        nc.scalar.dma_start(out=omega_row[0:1, :], in_=omega.rearrange("(o k) -> o k", o=1))
+        nc.scalar.dma_start(out=omega_c[:], in_=omega.rearrange("(g p t) -> p g t", g=2, t=PACK))
+        sources = {"phi": phi, "a": a, "y": y}
+        for key in LOADS:
+            load(key, sources[key[0]], key[1])
+        nc.vector.tensor_scalar(out=omega_s[:], in0=omega_c[:], scalar1=ROOT, scalar2=None, op0=MULT)
+
+        def omega_mm(c):
+            banks["omega", c] = bank()
+            nc.tensor.matmul(out=banks["omega", c][:], lhsT=ones[:], rhs=omega_row[:, c * HALF:(c + 1) * HALF], start=True, stop=True)
+
+        def omega_out(c):
+            nc.scalar.copy(out=omega_b[:, c * HALF:(c + 1) * HALF], in_=banks["omega", c][:])
+
+        def s1_mm(name, kg, c, block):
+            b = bank()
+            banks[name, kg, c, block] = b
+            cols = slice(block * P, (block + 1) * P)
+            b4 = b[:].rearrange("p (t n) -> p t n", t=PACK)
+            for t in range(PACK):
+                ks = slice(t * P, (t + 1) * P)
+                for g in range(2):
+                    nc.tensor.matmul_mx(
+                        out=b4[:, t, :],
+                        lhsT=codes["phi", g, kg][:, ks].bitcast(FP8X4),
+                        lhsT_scale=scales["phi", g, kg][:, ks],
+                        rhs=codes[name, g, c][:, cols].bitcast(FP8X4),
+                        rhs_scale=scales[name, g, c][:, cols],
+                        start=(g == 0),
+                        stop=(g == 1),
+                    )
+
+        def s1_out(name, kg, c, block):
+            cols = slice(block * P, (block + 1) * P)
+            key = ("g" + name, kg, c)
+            if key not in group:
+                group[key] = work.tile([P, HALF * PACK], BF16, name="gg", tag="g" + name, bufs=GB, align_bytes=64)
+            dst = group[key][:].rearrange("p (n t) -> p n t", t=PACK)[:, cols, :]
+            src = banks[name, kg, c, block][:].rearrange("p (t n) -> p n t", t=PACK)
+            if name == "y":
+                nc.scalar.activation(out=dst, in_=src, func=COPY, scale=ROOT)
+            else:
+                w = omega_s[:, kg, :].unsqueeze(1).to_broadcast([P, P, PACK])
+                nc.vector.tensor_tensor(out=dst, in0=src, in1=w, op=MULT)
+
+        def square(g, c):
+            nc.scalar.activation(out=sq[g][:, :, c * HALF:(c + 1) * HALF], in_=raw["phi", g, c][:], func=SQUARE)
+
+        def hsum(g, j):
+            nc.vector.scalar_tensor_tensor(
+                out=sq[g][:, j, :], in0=sq[g][:, j, :], scalar=-1.0 / N, in1=omega_b[:],
+                op0=MULT, op1=MULT, accum_out=hneg[:, g, j:j + 1],
+            )
+
+        def weigh(g, c):
+            t = work.tile([P, PACK, HALF], BF16, name="ah", tag="ah", bufs=2, align_bytes=64)
+            for j in range(PACK):
+                nc.vector.tensor_scalar(out=t[:, j, :], in0=raw["a", g, c][:, j, :], scalar1=hneg[:, g, j:j + 1], scalar2=None, op0=MULT)
+            raw["ah", g, c] = t
+
+        def product(pg, c, t, diagonal):
+            left, right = ("ah", "y") if diagonal else ("ga", "gy")
+            if not diagonal:
+                banks[pg, c, t] = bank()
+            ps = slice(t * P, (t + 1) * P)
+            for g in range(2):
+                nc.tensor.matmul_mx(
+                    out=banks[pg, c, t][:],
+                    lhsT=codes[left, g, pg][:, ps].bitcast(FP8X4),
+                    lhsT_scale=scales[left, g, pg][:, ps],
+                    rhs=codes[right, g, c][:].bitcast(FP8X4),
+                    rhs_scale=scales[right, g, c][:],
+                    start=(not diagonal and g == 0),
+                    stop=(diagonal and g == 1),
+                )
+
+        def evacuate(pg, c, t):
+            if (pg, c) not in outf:
+                outf[pg, c] = work.tile([P, PACK, HALF], F32, name="outf", tag="outf", bufs=3, align_bytes=64)
+            f = outf[pg, c]
+            nc.scalar.activation(out=f[:, t, :], in_=banks[pg, c, t][:], func=COPY, scale=ROOT)
+            done = [k for k in evacuated if k[:2] == (pg, c)]
+            evacuated.append((pg, c, t))
+            if len(done) == PACK - 1:
+                dst = out_0[pg * HALF:(pg + 1) * HALF, c * HALF:(c + 1) * HALF]
+                nc.sync.dma_start(out=dst.rearrange("(p t) m -> p t m", t=PACK), in_=f[:])
+
+        evacuated = []
+
+        def plane_mix(pg, c):
+            t = work.tile([P, HALF * PACK], BF16, name="og", tag="grp", bufs=6, align_bytes=64)
+            nc.vector.tensor_copy(out=t[:].rearrange("p (n t) -> p n t", t=PACK), in_=outf[pg, c][:].rearrange("p t n -> p n t"))
+            og[pg, c] = t
+
+        def plane_out(pg, c):
+            key = ("o", pg, c)
+            quantize(key, og[pg, c])
+            words = out_1[pg].rearrange("p m t -> p (m t)").bitcast(I32)
+            nc.sync.dma_start(out=words[:, c * HALF:(c + 1) * HALF], in_=codes[key][:].bitcast(I32))
+            srows = out_2[pg].bitcast(I32)
+            for q in range(4):
+                nc.sync.dma_start(
+                    out=srows[4 * q:4 * q + 4, c * P:(c + 1) * P],
+                    in_=scales[key][32 * q:32 * q + 4, :].bitcast(I32),
+                )
+
+        def step(head, *digits):
+            if head == "omb":
+                omega_mm(*digits)
+            elif head == "ob":
+                omega_out(*digits)
+            elif head.startswith("il_"):
+                key = (head[3:], digits[0], digits[1])
+                interleave(S if key in ON_SCALAR else V, key, key[0] == "y")
+            elif head.startswith("Q_"):
+                quantize((head[2:], digits[0], digits[1]))
+            elif head.startswith("Qg"):
+                quantize((head[1:], digits[0], digits[1]))
+            elif head == "sq":
+                square(*digits)
+            elif head == "hs":
+                hsum(*digits)
+            elif head == "wt_":
+                weigh(*digits)
+            elif head in ("my", "ma"):
+                s1_mm(head[1], *digits)
+            elif head in ("ey", "ea"):
+                s1_out(head[1], *digits)
+            elif head in ("f", "d"):
+                product(digits[0], digits[1], digits[2], head == "d")
+            elif head == "v":
+                evacuate(*digits)
+            elif head == "oi":
+                plane_mix(*digits)
+            elif head == "oq":
+                plane_out(*digits)
+            else:
+                raise ValueError(head)
+
+        for entry in ORDER:
+            step(*entry)

@@ -22,7 +22,7 @@ ROOT = 1.0 / 32.0
 GB = 3
 LOADS = [('phi', 0, 0), ('y', 0, 0), ('phi', 1, 0), ('y', 1, 0), ('phi', 0, 1), ('phi', 1, 1), ('a', 0, 0), ('a', 1, 0), ('y', 0, 1), ('y', 1, 1), ('a', 0, 1), ('a', 1, 1)]
 ON_SCALAR = [('y', 0, 0), ('y', 0, 1), ('y', 1, 0), ('y', 1, 1), ('a', 0, 1), ('a', 1, 1), ('ah', 0, 1), ('ah', 1, 1)]
-ORDER = [("omb", 1), ("omb", 0), ("ob", 1), ("ob", 0), ("il_phi", 0, 0), ("sq", 0, 0), ("Q_phi", 0, 0), ("il_y", 0, 0), ("il_phi", 1, 0), ("Q_phi", 1, 0), ("il_y", 1, 0), ("il_phi", 0, 1), ("Q_y", 0, 0), ("il_phi", 1, 1), ("sq", 0, 1), ("Q_y", 1, 0), ("il_a", 1, 0), ("my", 0, 0, 0), ("sq", 1, 1), ("my", 0, 0, 1), ("my", 0, 0, 2), ("hs", 0, 3), ("my", 0, 0, 3), ("Q_phi", 1, 1), ("ey", 0, 0, 0), ("hs", 0, 2), ("il_a", 0, 1), ("Q_a", 1, 0), ("il_a", 0, 0), ("il_a", 1, 1), ("hs", 0, 0), ("Q_a", 0, 0), ("hs", 0, 1), ("ma", 0, 0, 0), ("ey", 0, 0, 1), ("ma", 0, 0, 1), ("ey", 0, 0, 2), ("Q_a", 1, 1), ("ma", 0, 0, 2), ("ey", 0, 0, 3), ("wt_", 0, 1), ("ma", 0, 0, 3), ("il_y", 1, 1), ("Qgy", 0, 0), ("Q_phi", 0, 1), ("wt_", 0, 0), ("my", 1, 0, 0), ("Q_a", 0, 1), ("my", 1, 0, 1), ("ey", 1, 0, 0), ("ea", 0, 0, 0), ("ma", 0, 1, 0), ("ey", 1, 0, 1), ("Q_y", 1, 1), ("ma", 0, 1, 1), ("il_y", 0, 1), ("ea", 0, 1, 0), ("ma", 0, 1, 2), ("ea", 0, 1, 1), ("ma", 0, 1, 3), ("ea", 0, 1, 2), ("ma", 1, 1, 0), ("ea", 0, 1, 3), ("ma", 1, 1, 1), ("ea", 1, 1, 0), ("sq", 1, 0), ("ma", 1, 1, 2), ("Q_y", 0, 1), ("ma", 1, 1, 3), ("ea", 1, 1, 1), ("my", 0, 1, 0), ("ea", 1, 1, 2), ("ea", 1, 1, 3), ("my", 0, 1, 1), ("il_ah", 0, 1), ("hs", 1, 2), ("my", 0, 1, 2), ("my", 0, 1, 3), ("hs", 1, 3), ("my", 1, 0, 2), ("ey", 0, 1, 0), ("hs", 1, 1), ("ey", 0, 1, 1), ("my", 1, 0, 3), ("ey", 0, 1, 2), ("my", 1, 1, 0), ("Qga", 1, 1), ("ey", 0, 1, 3), ("my", 1, 1, 1), ("hs", 1, 0), ("ey", 1, 1, 0), ("my", 1, 1, 2), ("ey", 1, 1, 1), ("my", 1, 1, 3), ("Qgy", 0, 1), ("ey", 1, 1, 2), ("ma", 1, 0, 0), ("wt_", 1, 1), ("ey", 1, 1, 3), ("ma", 1, 0, 1), ("Qga", 0, 1), ("ey", 1, 0, 2), ("ma", 1, 0, 2), ("Qgy", 1, 1), ("il_ah", 1, 1), ("ma", 1, 0, 3), ("ea", 0, 0, 1), ("ea", 0, 0, 2), ("f", 1, 1, 0), ("f", 1, 1, 1), ("ea", 0, 0, 3), ("f", 1, 1, 2), ("Q_ah", 0, 1), ("ey", 1, 0, 3), ("Q_ah", 1, 1), ("f", 1, 1, 3), ("Qgy", 1, 0), ("d", 1, 1, 0), ("Qga", 0, 0), ("d", 1, 1, 1), ("v", 1, 1, 0), ("ea", 1, 0, 0), ("d", 1, 1, 2), ("v", 1, 1, 1), ("ea", 1, 0, 1), ("d", 1, 1, 3), ("v", 1, 1, 2), ("ea", 1, 0, 2), ("f", 1, 0, 0), ("v", 1, 1, 3), ("ea", 1, 0, 3), ("f", 1, 0, 1), ("oi", 1, 1), ("f", 1, 0, 2), ("f", 1, 0, 3), ("d", 1, 0, 0), ("Qga", 1, 0), ("d", 1, 0, 1), ("oq", 1, 1), ("v", 1, 0, 0), ("f", 0, 1, 0), ("v", 1, 0, 1), ("wt_", 1, 0), ("f", 0, 1, 1), ("il_ah", 0, 0), ("f", 0, 1, 2), ("f", 0, 1, 3), ("il_ah", 1, 0), ("d", 1, 0, 2), ("d", 1, 0, 3), ("v", 1, 0, 2), ("f", 0, 0, 0), ("v", 1, 0, 3), ("Q_ah", 0, 0), ("f", 0, 0, 1), ("Q_ah", 1, 0), ("f", 0, 0, 2), ("oi", 1, 0), ("d", 0, 1, 0), ("d", 0, 1, 1), ("v", 0, 1, 0), ("oq", 1, 0), ("d", 0, 1, 2), ("v", 0, 1, 1), ("d", 0, 1, 3), ("v", 0, 1, 2), ("f", 0, 0, 3), ("v", 0, 1, 3), ("d", 0, 0, 0), ("oi", 0, 1), ("d", 0, 0, 1), ("v", 0, 0, 0), ("d", 0, 0, 2), ("v", 0, 0, 1), ("d", 0, 0, 3), ("oq", 0, 1), ("v", 0, 0, 2), ("v", 0, 0, 3), ("oi", 0, 0), ("oq", 0, 0)]
+ORDER = [('omb', 1), ('omb', 0), ('ob', 0), ('ob', 1), ('il_phi', 0, 0), ('sq', 0, 0), ('Q_phi', 0, 0), ('il_y', 0, 0), ('il_phi', 1, 0), ('Q_phi', 1, 0), ('il_y', 1, 0), ('Q_y', 0, 0), ('il_phi', 0, 1), ('il_phi', 1, 1), ('sq', 1, 0), ('Q_phi', 0, 1), ('Q_y', 1, 0), ('sq', 1, 1), ('Q_phi', 1, 1), ('my', 0, 0, 0), ('il_a', 1, 0), ('my', 0, 0, 1), ('my', 0, 0, 2), ('il_a', 0, 0), ('my', 0, 0, 3), ('il_y', 0, 1), ('my', 1, 0, 0), ('my', 1, 0, 1), ('hs', 1, 3), ('my', 1, 0, 2), ('Q_a', 1, 0), ('my', 1, 0, 3), ('il_a', 0, 1), ('Q_a', 0, 0), ('hs', 1, 1), ('hs', 1, 0), ('il_a', 1, 1), ('Q_a', 0, 1), ('hs', 1, 2), ('ey', 0, 0, 0), ('Q_y', 0, 1), ('ma', 0, 0, 0), ('ey', 0, 0, 1), ('wt_', 1, 1), ('ey', 0, 0, 2), ('ma', 0, 0, 1), ('Q_a', 1, 1), ('ey', 0, 0, 3), ('ma', 0, 0, 2), ('ea', 0, 0, 0), ('il_ah', 1, 1), ('ma', 0, 1, 0), ('Qgy', 0, 0), ('ea', 0, 0, 1), ('ma', 0, 1, 1), ('ea', 0, 1, 0), ('ma', 0, 1, 2), ('ea', 0, 1, 1), ('ma', 0, 1, 3), ('ea', 0, 1, 2), ('il_y', 1, 1), ('ma', 0, 0, 3), ('ea', 0, 1, 3), ('ma', 1, 1, 0), ('Q_ah', 1, 1), ('ma', 1, 1, 1), ('ea', 1, 1, 0), ('ma', 1, 1, 2), ('ea', 1, 1, 1), ('sq', 0, 1), ('Qga', 0, 1), ('ma', 1, 1, 3), ('ea', 1, 1, 2), ('ma', 1, 0, 0), ('ea', 1, 1, 3), ('Q_y', 1, 1), ('ma', 1, 0, 1), ('ey', 1, 0, 0), ('hs', 0, 0), ('ey', 1, 0, 1), ('my', 1, 1, 0), ('ey', 1, 0, 2), ('my', 1, 1, 1), ('hs', 0, 1), ('ey', 1, 1, 0), ('my', 1, 1, 2), ('ey', 1, 1, 1), ('my', 1, 1, 3), ('hs', 0, 2), ('ey', 1, 1, 2), ('my', 0, 1, 0), ('ey', 1, 1, 3), ('my', 0, 1, 1), ('Qga', 1, 1), ('ey', 0, 1, 0), ('my', 0, 1, 2), ('Qgy', 1, 1), ('ey', 0, 1, 1), ('my', 0, 1, 3), ('hs', 0, 3), ('ey', 1, 0, 3), ('ma', 1, 0, 2), ('ey', 0, 1, 2), ('ma', 1, 0, 3), ('ey', 0, 1, 3), ('Qgy', 1, 0), ('wt_', 0, 1), ('f', 1, 0, 0), ('ea', 0, 0, 2), ('f', 1, 0, 1), ('il_ah', 0, 1), ('ea', 0, 0, 3), ('f', 1, 0, 2), ('Qgy', 0, 1), ('f', 1, 0, 3), ('ea', 1, 0, 0), ('f', 1, 1, 0), ('ea', 1, 0, 1), ('f', 1, 1, 1), ('Q_ah', 0, 1), ('ea', 1, 0, 2), ('d', 1, 0, 0), ('ea', 1, 0, 3), ('f', 1, 1, 2), ('v', 1, 0, 0), ('Qga', 0, 0), ('f', 1, 1, 3), ('Qga', 1, 0), ('d', 1, 0, 1), ('wt_', 0, 0), ('d', 1, 0, 2), ('v', 1, 0, 1), ('d', 1, 0, 3), ('wt_', 1, 0), ('v', 1, 0, 2), ('d', 1, 1, 0), ('il_ah', 0, 0), ('v', 1, 0, 3), ('d', 1, 1, 1), ('v', 1, 1, 0), ('d', 1, 1, 2), ('v', 1, 1, 1), ('il_ah', 1, 0), ('d', 1, 1, 3), ('v', 1, 1, 2), ('f', 0, 0, 0), ('v', 1, 1, 3), ('f', 0, 0, 1), ('Q_ah', 0, 0), ('f', 0, 0, 2), ('Q_ah', 1, 0), ('f', 0, 0, 3), ('oi', 1, 0), ('d', 0, 0, 0), ('d', 0, 0, 1), ('v', 0, 0, 0), ('oi', 1, 1), ('d', 0, 0, 2), ('v', 0, 0, 1), ('d', 0, 0, 3), ('v', 0, 0, 2), ('oq', 1, 0), ('f', 0, 1, 0), ('v', 0, 0, 3), ('f', 0, 1, 1), ('oq', 1, 1), ('d', 0, 1, 0), ('oi', 0, 0), ('d', 0, 1, 1), ('v', 0, 1, 0), ('f', 0, 1, 2), ('v', 0, 1, 1), ('oq', 0, 0), ('f', 0, 1, 3), ('d', 0, 1, 2), ('d', 0, 1, 3), ('v', 0, 1, 2), ('v', 0, 1, 3), ('oi', 0, 1), ('oq', 0, 1)]
 
 
 def tile_secondorderinfluenceustatisticmatrix_x1_kernel(tc, a, y, phi, omega, out_0, out_1, out_2):
@@ -48,15 +48,41 @@ def tile_secondorderinfluenceustatisticmatrix_x1_kernel(tc, a, y, phi, omega, ou
             nc.sync.dma_start(out=t[:], in_=rows.rearrange("(p j) w -> p j w", j=PACK))
             raw[key] = t
 
-        def permuted(t):
-            return t[:].rearrange("p j (m t) -> p t m j", t=PACK)
+        def mix_phi(t, src):
+            nc.vector.tensor_copy(
+                out=t.rearrange("p (t b r j) -> p t b r j", t=PACK, b=16, j=PACK),
+                in_=src.rearrange("p j (b t r) -> p t b r j", b=16, t=PACK),
+            )
 
-        def interleave(engine_copy, key, natural):
+        def mix_a_vector(t, src):
+            nc.vector.tensor_copy(
+                out=t.rearrange("p (t m n j) -> p m t n j", t=PACK, n=2, j=PACK),
+                in_=src.rearrange("p j (m n t) -> p m t n j", n=2, t=PACK),
+            )
+
+        def mix_a_scalar(t, src):
+            nc.scalar.copy(
+                out=t.rearrange("p (t m j) -> p m j t", t=PACK, j=PACK),
+                in_=src.rearrange("p j (m t) -> p m j t", t=PACK),
+            )
+
+        def mix_plain(copy, t, src):
+            copy(
+                out=t.rearrange("p (c i j) -> p c j i", i=4, j=PACK),
+                in_=src.rearrange("p j (c i) -> p c j i", i=4),
+            )
+
+        def interleave(key):
             t = work.tile([P, HALF * PACK], BF16, name="grp", tag="grp", bufs=6, align_bytes=64)
-            if natural:
-                engine_copy(out=t[:].rearrange("p (c j) -> p c j", j=PACK), in_=raw[key][:].rearrange("p j c -> p c j"))
+            src = raw[key][:]
+            if key[0] == "y":
+                mix_plain(nc.scalar.copy if key in ON_SCALAR else nc.vector.tensor_copy, t[:], src)
+            elif key[0] == "phi":
+                mix_phi(t[:], src)
+            elif key in ON_SCALAR:
+                mix_a_scalar(t[:], src)
             else:
-                engine_copy(out=t[:].rearrange("p (t m j) -> p t m j", t=PACK, j=PACK), in_=permuted(raw[key]))
+                mix_a_vector(t[:], src)
             group[key] = t
 
         def quantize(key, src=None):
@@ -69,7 +95,7 @@ def tile_secondorderinfluenceustatisticmatrix_x1_kernel(tc, a, y, phi, omega, ou
         omega_row = keep_tile([P, N], BF16, "omega_row")
         ones = keep_tile([P, P], BF16, "ones")
         omega_b = keep_tile([P, N], BF16, "omega_b")
-        omega_c = keep_tile([P, 2, PACK], BF16, "omega_c")
+        omega_p = keep_tile([P, N], BF16, "omega_p")
         omega_s = keep_tile([P, 2, PACK], F32, "omega_s")
         hneg = keep_tile([P, 2, PACK], F32, "hneg")
         sq = [keep_tile([P, PACK, N], F32, "sq%d" % g) for g in range(2)]
@@ -80,17 +106,23 @@ def tile_secondorderinfluenceustatisticmatrix_x1_kernel(tc, a, y, phi, omega, ou
         banks = {}
         outf = {}
         og = {}
-        V = nc.vector.tensor_copy
-        S = nc.scalar.copy
 
         nc.vector.memset(omega_row[:], 0.0)
         nc.vector.memset(ones[:], 1.0)
         nc.scalar.dma_start(out=omega_row[0:1, :], in_=omega.rearrange("(o k) -> o k", o=1))
-        nc.scalar.dma_start(out=omega_c[:], in_=omega.rearrange("(g p t) -> p g t", g=2, t=PACK))
         sources = {"phi": phi, "a": a, "y": y}
         for key in LOADS:
             load(key, sources[key[0]], key[1])
-        nc.vector.tensor_scalar(out=omega_s[:], in0=omega_c[:], scalar1=ROOT, scalar2=None, op0=MULT)
+        nc.vector.tensor_copy(
+            out=omega_p[:].rearrange("p (g t b r) -> p g t b r", g=2, t=PACK, b=16),
+            in_=omega_row[:].rearrange("p (g b t r) -> p g t b r", g=2, b=16, t=PACK),
+        )
+        spread = bank()
+        for g in range(2):
+            for t in range(PACK):
+                ks = slice((g * PACK + t) * P, (g * PACK + t + 1) * P)
+                nc.tensor.matmul(out=spread[:, g * PACK + t:g * PACK + t + 1], lhsT=omega_p[:, ks], rhs=ones[:, 0:1], start=True, stop=True)
+        nc.scalar.activation(out=omega_s[:], in_=spread[:, :2 * PACK].rearrange("p (g t) -> p g t", g=2), func=COPY, scale=ROOT)
 
         def omega_mm(c):
             banks["omega", c] = bank()
@@ -166,17 +198,13 @@ def tile_secondorderinfluenceustatisticmatrix_x1_kernel(tc, a, y, phi, omega, ou
                 outf[pg, c] = work.tile([P, PACK, HALF], F32, name="outf", tag="outf", bufs=3, align_bytes=64)
             f = outf[pg, c]
             nc.scalar.activation(out=f[:, t, :], in_=banks[pg, c, t][:], func=COPY, scale=ROOT)
-            done = [k for k in evacuated if k[:2] == (pg, c)]
-            evacuated.append((pg, c, t))
-            if len(done) == PACK - 1:
-                dst = out_0[pg * HALF:(pg + 1) * HALF, c * HALF:(c + 1) * HALF]
-                nc.sync.dma_start(out=dst.rearrange("(p t) m -> p t m", t=PACK), in_=f[:])
-
-        evacuated = []
+            if t % 2:
+                dst = out_0[pg * HALF:(pg + 1) * HALF, c * HALF:(c + 1) * HALF].rearrange("(p t) m -> p t m", t=PACK)
+                nc.sync.dma_start(out=dst[:, t - 1:t + 1, :], in_=f[:, t - 1:t + 1, :])
 
         def plane_mix(pg, c):
             t = work.tile([P, HALF * PACK], BF16, name="og", tag="grp", bufs=6, align_bytes=64)
-            nc.vector.tensor_copy(out=t[:].rearrange("p (n t) -> p n t", t=PACK), in_=outf[pg, c][:].rearrange("p t n -> p n t"))
+            mix_plain(nc.vector.tensor_copy, t[:], outf[pg, c][:])
             og[pg, c] = t
 
         def plane_out(pg, c):
@@ -198,7 +226,7 @@ def tile_secondorderinfluenceustatisticmatrix_x1_kernel(tc, a, y, phi, omega, ou
                 omega_out(*digits)
             elif head.startswith("il_"):
                 key = (head[3:], digits[0], digits[1])
-                interleave(S if key in ON_SCALAR else V, key, key[0] == "y")
+                interleave(key)
             elif head.startswith("Q_"):
                 quantize((head[2:], digits[0], digits[1]))
             elif head.startswith("Qg"):

@@ -1,6 +1,7 @@
 from contextlib import ExitStack
 
 import concourse.mybir as mybir
+from concourse.masks import make_identity
 
 N = 1024
 FLOPS = 4 * 2 * N * N * N
@@ -19,10 +20,10 @@ P = 128
 PACK = 4
 HALF = 512
 ROOT = 1.0 / 32.0
-GB = 3
+CHUNKS = 24
 LOADS = [('phi', 0, 0), ('y', 0, 0), ('phi', 1, 0), ('y', 1, 0), ('phi', 0, 1), ('phi', 1, 1), ('a', 0, 0), ('a', 1, 0), ('y', 0, 1), ('y', 1, 1), ('a', 0, 1), ('a', 1, 1)]
-ON_SCALAR = [('y', 0, 0), ('y', 0, 1), ('y', 1, 0), ('y', 1, 1), ('a', 0, 1), ('a', 1, 1), ('ah', 0, 1), ('ah', 1, 1)]
-ORDER = [('omb', 1), ('omb', 0), ('ob', 0), ('ob', 1), ('il_phi', 0, 0), ('sq', 0, 0), ('Q_phi', 0, 0), ('il_y', 0, 0), ('il_phi', 1, 0), ('Q_phi', 1, 0), ('il_y', 1, 0), ('Q_y', 0, 0), ('il_phi', 0, 1), ('il_phi', 1, 1), ('sq', 1, 0), ('Q_phi', 0, 1), ('Q_y', 1, 0), ('sq', 1, 1), ('Q_phi', 1, 1), ('my', 0, 0, 0), ('il_a', 1, 0), ('my', 0, 0, 1), ('my', 0, 0, 2), ('il_a', 0, 0), ('my', 0, 0, 3), ('il_y', 0, 1), ('my', 1, 0, 0), ('my', 1, 0, 1), ('hs', 1, 3), ('my', 1, 0, 2), ('Q_a', 1, 0), ('my', 1, 0, 3), ('il_a', 0, 1), ('Q_a', 0, 0), ('hs', 1, 1), ('hs', 1, 0), ('il_a', 1, 1), ('Q_a', 0, 1), ('hs', 1, 2), ('ey', 0, 0, 0), ('Q_y', 0, 1), ('ma', 0, 0, 0), ('ey', 0, 0, 1), ('wt_', 1, 1), ('ey', 0, 0, 2), ('ma', 0, 0, 1), ('Q_a', 1, 1), ('ey', 0, 0, 3), ('ma', 0, 0, 2), ('ea', 0, 0, 0), ('il_ah', 1, 1), ('ma', 0, 1, 0), ('Qgy', 0, 0), ('ea', 0, 0, 1), ('ma', 0, 1, 1), ('ea', 0, 1, 0), ('ma', 0, 1, 2), ('ea', 0, 1, 1), ('ma', 0, 1, 3), ('ea', 0, 1, 2), ('il_y', 1, 1), ('ma', 0, 0, 3), ('ea', 0, 1, 3), ('ma', 1, 1, 0), ('Q_ah', 1, 1), ('ma', 1, 1, 1), ('ea', 1, 1, 0), ('ma', 1, 1, 2), ('ea', 1, 1, 1), ('sq', 0, 1), ('Qga', 0, 1), ('ma', 1, 1, 3), ('ea', 1, 1, 2), ('ma', 1, 0, 0), ('ea', 1, 1, 3), ('Q_y', 1, 1), ('ma', 1, 0, 1), ('ey', 1, 0, 0), ('hs', 0, 0), ('ey', 1, 0, 1), ('my', 1, 1, 0), ('ey', 1, 0, 2), ('my', 1, 1, 1), ('hs', 0, 1), ('ey', 1, 1, 0), ('my', 1, 1, 2), ('ey', 1, 1, 1), ('my', 1, 1, 3), ('hs', 0, 2), ('ey', 1, 1, 2), ('my', 0, 1, 0), ('ey', 1, 1, 3), ('my', 0, 1, 1), ('Qga', 1, 1), ('ey', 0, 1, 0), ('my', 0, 1, 2), ('Qgy', 1, 1), ('ey', 0, 1, 1), ('my', 0, 1, 3), ('hs', 0, 3), ('ey', 1, 0, 3), ('ma', 1, 0, 2), ('ey', 0, 1, 2), ('ma', 1, 0, 3), ('ey', 0, 1, 3), ('Qgy', 1, 0), ('wt_', 0, 1), ('f', 1, 0, 0), ('ea', 0, 0, 2), ('f', 1, 0, 1), ('il_ah', 0, 1), ('ea', 0, 0, 3), ('f', 1, 0, 2), ('Qgy', 0, 1), ('f', 1, 0, 3), ('ea', 1, 0, 0), ('f', 1, 1, 0), ('ea', 1, 0, 1), ('f', 1, 1, 1), ('Q_ah', 0, 1), ('ea', 1, 0, 2), ('d', 1, 0, 0), ('ea', 1, 0, 3), ('f', 1, 1, 2), ('v', 1, 0, 0), ('Qga', 0, 0), ('f', 1, 1, 3), ('Qga', 1, 0), ('d', 1, 0, 1), ('wt_', 0, 0), ('d', 1, 0, 2), ('v', 1, 0, 1), ('d', 1, 0, 3), ('wt_', 1, 0), ('v', 1, 0, 2), ('d', 1, 1, 0), ('il_ah', 0, 0), ('v', 1, 0, 3), ('d', 1, 1, 1), ('v', 1, 1, 0), ('d', 1, 1, 2), ('v', 1, 1, 1), ('il_ah', 1, 0), ('d', 1, 1, 3), ('v', 1, 1, 2), ('f', 0, 0, 0), ('v', 1, 1, 3), ('f', 0, 0, 1), ('Q_ah', 0, 0), ('f', 0, 0, 2), ('Q_ah', 1, 0), ('f', 0, 0, 3), ('oi', 1, 0), ('d', 0, 0, 0), ('d', 0, 0, 1), ('v', 0, 0, 0), ('oi', 1, 1), ('d', 0, 0, 2), ('v', 0, 0, 1), ('d', 0, 0, 3), ('v', 0, 0, 2), ('oq', 1, 0), ('f', 0, 1, 0), ('v', 0, 0, 3), ('f', 0, 1, 1), ('oq', 1, 1), ('d', 0, 1, 0), ('oi', 0, 0), ('d', 0, 1, 1), ('v', 0, 1, 0), ('f', 0, 1, 2), ('v', 0, 1, 1), ('oq', 0, 0), ('f', 0, 1, 3), ('d', 0, 1, 2), ('d', 0, 1, 3), ('v', 0, 1, 2), ('v', 0, 1, 3), ('oi', 0, 1), ('oq', 0, 1)]
+ON_SCALAR = [('y', 0, 1), ('y', 1, 1), ('a', 0, 1), ('a', 1, 1), ('ah', 0, 0), ('ah', 0, 1), ('ah', 1, 1)]
+ORDER = [('il_phi', 0, 0), ('sq', 0, 0), ('omb', 0), ('omb', 1), ('omp',), ('pm_y', 0, 0, 0), ('Q_phi', 0, 0), ('pm_y', 0, 0, 1), ('ob', 0), ('omt',), ('pc_y', 0, 0, 0), ('il_phi', 1, 0), ('pc_y', 0, 0, 1), ('oms',), ('ob', 1), ('pm_y', 1, 0, 0), ('Q_y', 0, 0), ('sq', 1, 0), ('pm_y', 1, 0, 1), ('Q_phi', 1, 0), ('il_phi', 0, 1), ('sq', 0, 1), ('il_phi', 1, 1), ('Q_phi', 0, 1), ('pm_a', 0, 0, 0), ('Q_phi', 1, 1), ('pm_a', 0, 0, 1), ('pc_y', 1, 0, 1), ('hs', 0, 0), ('pc_a', 0, 0, 0), ('pm_a', 1, 0, 1), ('pc_a', 0, 0, 1), ('pm_a', 1, 0, 0), ('hs', 0, 1), ('pc_a', 1, 0, 1), ('pc_a', 1, 0, 0), ('hs', 0, 2), ('pc_y', 1, 0, 0), ('il_y', 0, 1), ('Q_a', 1, 0), ('Q_a', 0, 0), ('hs', 0, 3), ('ma', 0, 0, 3), ('ma', 1, 0, 1), ('il_a', 0, 1), ('Q_y', 1, 0), ('ma', 1, 0, 2), ('wt_', 0, 1), ('my', 1, 0, 3), ('ea', 0, 0, 3), ('ma', 1, 0, 3), ('ea', 1, 0, 1), ('ma', 1, 0, 0), ('il_a', 1, 1), ('ea', 1, 0, 3), ('my', 1, 0, 0), ('Q_a', 0, 1), ('ma', 0, 0, 0), ('ea', 1, 0, 0), ('my', 1, 0, 2), ('Q_y', 0, 1), ('my', 1, 0, 1), ('ea', 0, 0, 0), ('ey', 1, 0, 0), ('ma', 0, 0, 2), ('Q_a', 1, 1), ('il_y', 1, 1), ('ea', 1, 0, 2), ('ma', 0, 0, 1), ('ea', 0, 0, 2), ('ma', 1, 1, 1), ('Qga', 1, 0), ('ma', 1, 1, 3), ('ea', 1, 1, 1), ('ma', 1, 1, 0), ('ey', 1, 0, 2), ('ea', 1, 1, 3), ('ma', 0, 1, 0), ('sq', 1, 1), ('Q_y', 1, 1), ('my', 0, 0, 0), ('ea', 0, 1, 0), ('my', 1, 1, 1), ('ea', 0, 0, 1), ('my', 1, 1, 0), ('ea', 1, 1, 0), ('ey', 1, 1, 1), ('my', 0, 1, 2), ('hs', 1, 2), ('ey', 1, 1, 0), ('my', 0, 1, 1), ('ey', 0, 1, 2), ('my', 1, 1, 3), ('hs', 1, 3), ('ey', 0, 1, 1), ('my', 0, 1, 0), ('ey', 0, 0, 0), ('Qga', 0, 0), ('my', 0, 0, 1), ('ey', 1, 1, 3), ('hs', 1, 1), ('my', 0, 0, 3), ('ey', 0, 1, 0), ('ey', 0, 0, 1), ('ma', 1, 1, 2), ('hs', 1, 0), ('ey', 0, 0, 3), ('my', 0, 0, 2), ('ey', 1, 0, 3), ('ma', 0, 1, 3), ('ey', 0, 0, 2), ('wt_', 0, 0), ('my', 0, 1, 3), ('ey', 1, 0, 1), ('wt_', 1, 0), ('ma', 0, 1, 1), ('il_ah', 0, 0), ('Qgy', 0, 0), ('ma', 0, 1, 2), ('Qgy', 1, 0), ('my', 1, 1, 2), ('il_ah', 1, 0), ('f', 0, 0, 2), ('f', 0, 0, 1), ('ey', 1, 1, 2), ('Q_ah', 0, 0), ('ey', 0, 1, 3), ('f', 0, 0, 3), ('Q_ah', 1, 0), ('il_ah', 0, 1), ('f', 0, 0, 0), ('ea', 0, 1, 2), ('d', 0, 0, 3), ('wt_', 1, 1), ('d', 0, 0, 2), ('Qgy', 1, 1), ('d', 0, 0, 0), ('Qgy', 0, 1), ('d', 0, 0, 1), ('v', 0, 0, 0), ('ea', 0, 1, 1), ('f', 0, 1, 2), ('v', 0, 0, 1), ('Q_ah', 0, 1), ('f', 0, 1, 1), ('v', 0, 0, 3), ('ea', 0, 1, 3), ('d', 0, 1, 2), ('v', 0, 0, 2), ('ea', 1, 1, 2), ('d', 0, 1, 1), ('il_ah', 1, 1), ('Qga', 0, 1), ('f', 0, 1, 0), ('Qga', 1, 1), ('f', 0, 1, 3), ('oi', 0, 0), ('f', 1, 0, 3), ('d', 0, 1, 3), ('v', 0, 1, 1), ('f', 1, 0, 0), ('Q_ah', 1, 1), ('f', 1, 0, 1), ('v', 0, 1, 3), ('oq', 0, 0), ('d', 1, 0, 0), ('v', 0, 1, 2), ('d', 1, 0, 1), ('v', 1, 0, 0), ('d', 1, 0, 3), ('v', 1, 0, 1), ('d', 0, 1, 0), ('v', 1, 0, 3), ('f', 1, 0, 2), ('v', 0, 1, 0), ('hf', 1, 1, 0, 0), ('oi', 0, 1), ('d', 1, 0, 2), ('hv', 1, 1, 0, 0), ('hf', 1, 1, 0, 1), ('v', 1, 0, 2), ('oq', 0, 1), ('oi', 1, 0), ('hf', 1, 1, 1, 0), ('hv', 1, 1, 0, 1), ('hi', 1, 1, 0), ('hf', 1, 1, 1, 1), ('hv', 1, 1, 1, 0), ('oq', 1, 0), ('hq', 1, 1, 0), ('hv', 1, 1, 1, 1), ('hi', 1, 1, 1), ('hq', 1, 1, 1)]
 
 
 def tile_secondorderinfluenceustatisticmatrix_x1_kernel(tc, a, y, phi, omega, out_0, out_1, out_2):
@@ -32,6 +33,9 @@ def tile_secondorderinfluenceustatisticmatrix_x1_kernel(tc, a, y, phi, omega, ou
         work = ctx.enter_context(tc.tile_pool(name="work", bufs=3))
         psum = ctx.enter_context(tc.psum_pool(name="psum", bufs=4))
         ctx.enter_context(tc.manual_schedule())
+
+        def chunk():
+            return work.tile([P, PACK * HALF], BF16, name="chunk", tag="chunk", bufs=CHUNKS, align_bytes=64)
 
         def keep_tile(shape, dtype, name):
             return keep.tile(shape, dtype, name=name, align_bytes=64)
@@ -43,9 +47,9 @@ def tile_secondorderinfluenceustatisticmatrix_x1_kernel(tc, a, y, phi, omega, ou
 
         def load(key, src, g):
             c = key[2]
-            t = keep_tile([P, PACK, HALF], BF16, "raw_%s_%d_%d" % key)
+            t = chunk()[:].rearrange("p (j w) -> p j w", j=PACK)
             rows = src[g * HALF:(g + 1) * HALF, c * HALF:(c + 1) * HALF]
-            nc.sync.dma_start(out=t[:], in_=rows.rearrange("(p j) w -> p j w", j=PACK))
+            nc.sync.dma_start(out=t, in_=rows.rearrange("(p j) w -> p j w", j=PACK))
             raw[key] = t
 
         def mix_phi(t, src):
@@ -73,8 +77,8 @@ def tile_secondorderinfluenceustatisticmatrix_x1_kernel(tc, a, y, phi, omega, ou
             )
 
         def interleave(key):
-            t = work.tile([P, HALF * PACK], BF16, name="grp", tag="grp", bufs=6, align_bytes=64)
-            src = raw[key][:]
+            t = chunk()
+            src = raw[key]
             if key[0] == "y":
                 mix_plain(nc.scalar.copy if key in ON_SCALAR else nc.vector.tensor_copy, t[:], src)
             elif key[0] == "phi":
@@ -104,25 +108,50 @@ def tile_secondorderinfluenceustatisticmatrix_x1_kernel(tc, a, y, phi, omega, ou
             return psum.tile([P, HALF], F32, name="bank", tag="bank", bufs=8)
 
         banks = {}
+        stored = set()
         outf = {}
         og = {}
 
         nc.vector.memset(omega_row[:], 0.0)
         nc.vector.memset(ones[:], 1.0)
-        nc.scalar.dma_start(out=omega_row[0:1, :], in_=omega.rearrange("(o k) -> o k", o=1))
         sources = {"phi": phi, "a": a, "y": y}
-        for key in LOADS:
+        for i, key in enumerate(LOADS):
             load(key, sources[key[0]], key[1])
-        nc.vector.tensor_copy(
-            out=omega_p[:].rearrange("p (g t b r) -> p g t b r", g=2, t=PACK, b=16),
-            in_=omega_row[:].rearrange("p (g b t r) -> p g t b r", g=2, b=16, t=PACK),
-        )
-        spread = bank()
-        for g in range(2):
-            for t in range(PACK):
-                ks = slice((g * PACK + t) * P, (g * PACK + t + 1) * P)
-                nc.tensor.matmul(out=spread[:, g * PACK + t:g * PACK + t + 1], lhsT=omega_p[:, ks], rhs=ones[:, 0:1], start=True, stop=True)
-        nc.scalar.activation(out=omega_s[:], in_=spread[:, :2 * PACK].rearrange("p (g t) -> p g t", g=2), func=COPY, scale=ROOT)
+            if i == 0:
+                nc.sync.dma_start(out=omega_row[0:1, :], in_=omega.rearrange("(o k) -> o k", o=1))
+        ident = keep_tile([P, P], BF16, "ident")
+        make_identity(nc, ident[:])
+
+        def turn(key, h):
+            b = psum.tile([P, 2 * HALF], BF16, name="bank", tag="bank", bufs=8)
+            banks["turn", key, h] = b
+            for i in range(2):
+                part = 2 * h + i
+                if key[0] == "y":
+                    rhs = raw[key][:, :, part * P:(part + 1) * P].rearrange("p j c -> p c j")
+                else:
+                    rhs = raw[key].rearrange("p j (m t) -> p t m j", t=PACK)[:, part, :, :]
+                nc.tensor.matmul(out=b[:, i * HALF:(i + 1) * HALF].rearrange("p (c j) -> p c j", j=PACK), lhsT=ident[:], rhs=rhs, start=True, stop=True)
+
+        def turn_out(key, h):
+            if key not in group:
+                group[key] = chunk()
+            nc.scalar.copy(out=group[key][:, h * 2 * HALF:(h + 1) * 2 * HALF], in_=banks["turn", key, h][:])
+
+        def omega_permute():
+            nc.vector.tensor_copy(
+                out=omega_p[:].rearrange("p (g t b r) -> p g t b r", g=2, t=PACK, b=16),
+                in_=omega_row[:].rearrange("p (g b t r) -> p g t b r", g=2, b=16, t=PACK),
+            )
+
+        def omega_turn():
+            spread = bank()
+            banks["spread"] = spread
+            for i in range(2 * PACK):
+                nc.tensor.matmul(out=spread[:, i:i + 1], lhsT=omega_p[:, i * P:(i + 1) * P], rhs=ones[:, 0:1], start=True, stop=True)
+
+        def omega_scale():
+            nc.scalar.activation(out=omega_s[:], in_=banks["spread"][:, :2 * PACK].rearrange("p (g t) -> p g t", g=2), func=COPY, scale=ROOT)
 
         def omega_mm(c):
             banks["omega", c] = bank()
@@ -153,7 +182,7 @@ def tile_secondorderinfluenceustatisticmatrix_x1_kernel(tc, a, y, phi, omega, ou
             cols = slice(block * P, (block + 1) * P)
             key = ("g" + name, kg, c)
             if key not in group:
-                group[key] = work.tile([P, HALF * PACK], BF16, name="gg", tag="g" + name, bufs=GB, align_bytes=64)
+                group[key] = chunk()
             dst = group[key][:].rearrange("p (n t) -> p n t", t=PACK)[:, cols, :]
             src = banks[name, kg, c, block][:].rearrange("p (t n) -> p n t", t=PACK)
             if name == "y":
@@ -163,7 +192,7 @@ def tile_secondorderinfluenceustatisticmatrix_x1_kernel(tc, a, y, phi, omega, ou
                 nc.vector.tensor_tensor(out=dst, in0=src, in1=w, op=MULT)
 
         def square(g, c):
-            nc.scalar.activation(out=sq[g][:, :, c * HALF:(c + 1) * HALF], in_=raw["phi", g, c][:], func=SQUARE)
+            nc.scalar.activation(out=sq[g][:, :, c * HALF:(c + 1) * HALF], in_=raw["phi", g, c], func=SQUARE)
 
         def hsum(g, j):
             nc.vector.scalar_tensor_tensor(
@@ -172,7 +201,7 @@ def tile_secondorderinfluenceustatisticmatrix_x1_kernel(tc, a, y, phi, omega, ou
             )
 
         def weigh(g, c):
-            t = work.tile([P, PACK, HALF], BF16, name="ah", tag="ah", bufs=2, align_bytes=64)
+            t = chunk()[:].rearrange("p (j w) -> p j w", j=PACK)
             for j in range(PACK):
                 nc.vector.tensor_scalar(out=t[:, j, :], in0=raw["a", g, c][:, j, :], scalar1=hneg[:, g, j:j + 1], scalar2=None, op0=MULT)
             raw["ah", g, c] = t
@@ -195,15 +224,17 @@ def tile_secondorderinfluenceustatisticmatrix_x1_kernel(tc, a, y, phi, omega, ou
 
         def evacuate(pg, c, t):
             if (pg, c) not in outf:
-                outf[pg, c] = work.tile([P, PACK, HALF], F32, name="outf", tag="outf", bufs=3, align_bytes=64)
+                outf[pg, c] = work.tile([P, PACK, HALF], F32, name="outf", tag="outf", bufs=4, align_bytes=64)
             f = outf[pg, c]
             nc.scalar.activation(out=f[:, t, :], in_=banks[pg, c, t][:], func=COPY, scale=ROOT)
-            if t % 2:
+            stored.add((pg, c, t))
+            if (pg, c, t ^ 1) in stored:
+                pair = slice(t - t % 2, t - t % 2 + 2)
                 dst = out_0[pg * HALF:(pg + 1) * HALF, c * HALF:(c + 1) * HALF].rearrange("(p t) m -> p t m", t=PACK)
-                nc.sync.dma_start(out=dst[:, t - 1:t + 1, :], in_=f[:, t - 1:t + 1, :])
+                nc.sync.dma_start(out=dst[:, pair, :], in_=f[:, pair, :])
 
         def plane_mix(pg, c):
-            t = work.tile([P, HALF * PACK], BF16, name="og", tag="grp", bufs=6, align_bytes=64)
+            t = chunk()
             mix_plain(nc.vector.tensor_copy, t[:], outf[pg, c][:])
             og[pg, c] = t
 
@@ -219,8 +250,64 @@ def tile_secondorderinfluenceustatisticmatrix_x1_kernel(tc, a, y, phi, omega, ou
                     in_=scales[key][32 * q:32 * q + 4, :].bitcast(I32),
                 )
 
+        def half_product(pg, c, h, u):
+            b = bank()
+            banks[pg, c, h, u] = b
+            cols = slice(h * 256, (h + 1) * 256)
+            for i in range(2):
+                t = 2 * u + i
+                ps = slice(t * P, (t + 1) * P)
+                for diagonal in (False, True):
+                    left, right = ("ah", "y") if diagonal else ("ga", "gy")
+                    for g in range(2):
+                        nc.tensor.matmul_mx(
+                            out=b[:, i * 256:(i + 1) * 256],
+                            lhsT=codes[left, g, pg][:, ps].bitcast(FP8X4),
+                            lhsT_scale=scales[left, g, pg][:, ps],
+                            rhs=codes[right, g, c][:, cols].bitcast(FP8X4),
+                            rhs_scale=scales[right, g, c][:, cols],
+                            start=(not diagonal and g == 0),
+                            stop=(diagonal and g == 1),
+                        )
+
+        def half_evacuate(pg, c, h, u):
+            if (pg, c) not in outf:
+                outf[pg, c] = work.tile([P, PACK, HALF], F32, name="outf", tag="outf", bufs=4, align_bytes=64)
+            f = outf[pg, c][:, 2 * u:2 * u + 2, h * 256:(h + 1) * 256]
+            nc.scalar.activation(out=f, in_=banks[pg, c, h, u][:].rearrange("p (t n) -> p t n", t=2), func=COPY, scale=ROOT)
+            rows = out_0[pg * HALF:(pg + 1) * HALF, c * HALF + h * 256:c * HALF + (h + 1) * 256].rearrange("(p t) m -> p t m", t=PACK)
+            nc.sync.dma_start(out=rows[:, 2 * u:2 * u + 2, :], in_=f)
+
+        def half_mix(pg, c, h):
+            t = chunk()
+            mix_plain(nc.vector.tensor_copy, t[:, :HALF * 2], outf[pg, c][:, :, h * 256:(h + 1) * 256])
+            og[pg, c, h] = t
+
+        def half_out(pg, c, h):
+            if ("o", pg, c) not in codes:
+                codes["o", pg, c] = keep_tile([P, HALF], U32, "codes_o_%d_%d" % (pg, c))
+                scales["o", pg, c] = keep_tile([P, HALF], U8, "scales_o_%d_%d" % (pg, c))
+            cols = slice(h * 256, (h + 1) * 256)
+            q = codes["o", pg, c][:, cols]
+            s = scales["o", pg, c][:, cols]
+            nc.vector.quantize_mx(out=q.bitcast(FP8X4), scales=s, in_=og[pg, c, h][:, :HALF * 2])
+            words = out_1[pg].rearrange("p m t -> p (m t)").bitcast(I32)
+            nc.sync.dma_start(out=words[:, c * HALF + h * 256:c * HALF + (h + 1) * 256], in_=q.bitcast(I32))
+            srows = out_2[pg].bitcast(I32)
+            for r in range(4):
+                nc.sync.dma_start(
+                    out=srows[4 * r:4 * r + 4, c * P + h * 64:c * P + (h + 1) * 64],
+                    in_=s[32 * r:32 * r + 4, :].bitcast(I32),
+                )
+
         def step(head, *digits):
-            if head == "omb":
+            if head == "omp":
+                omega_permute()
+            elif head == "omt":
+                omega_turn()
+            elif head == "oms":
+                omega_scale()
+            elif head == "omb":
                 omega_mm(*digits)
             elif head == "ob":
                 omega_out(*digits)
@@ -245,6 +332,18 @@ def tile_secondorderinfluenceustatisticmatrix_x1_kernel(tc, a, y, phi, omega, ou
                 product(digits[0], digits[1], digits[2], head == "d")
             elif head == "v":
                 evacuate(*digits)
+            elif head.startswith("pm_"):
+                turn((head[3:], digits[0], digits[1]), digits[2])
+            elif head.startswith("pc_"):
+                turn_out((head[3:], digits[0], digits[1]), digits[2])
+            elif head == "hf":
+                half_product(*digits)
+            elif head == "hv":
+                half_evacuate(*digits)
+            elif head == "hi":
+                half_mix(*digits)
+            elif head == "hq":
+                half_out(*digits)
             elif head == "oi":
                 plane_mix(*digits)
             elif head == "oq":

@@ -20,10 +20,9 @@ P = 128
 PACK = 4
 HALF = 512
 ROOT = 1.0 / 32.0
-CHUNKS = 24
-LOADS = [('phi', 0, 0), ('y', 0, 0), ('phi', 1, 0), ('y', 1, 0), ('phi', 0, 1), ('phi', 1, 1), ('a', 0, 0), ('a', 1, 0), ('y', 0, 1), ('y', 1, 1), ('a', 0, 1), ('a', 1, 1)]
-ON_SCALAR = [('y', 0, 1), ('y', 1, 1), ('a', 0, 1), ('a', 1, 1), ('ah', 0, 0), ('ah', 0, 1), ('ah', 1, 1)]
-ORDER = [('il_phi', 0, 0), ('sq', 0, 0), ('omb', 0), ('omb', 1), ('omp',), ('pm_y', 0, 0, 0), ('Q_phi', 0, 0), ('pm_y', 0, 0, 1), ('ob', 0), ('omt',), ('pc_y', 0, 0, 0), ('il_phi', 1, 0), ('pc_y', 0, 0, 1), ('oms',), ('ob', 1), ('pm_y', 1, 0, 0), ('Q_y', 0, 0), ('sq', 1, 0), ('pm_y', 1, 0, 1), ('Q_phi', 1, 0), ('il_phi', 0, 1), ('sq', 0, 1), ('il_phi', 1, 1), ('Q_phi', 0, 1), ('pm_a', 0, 0, 0), ('Q_phi', 1, 1), ('pm_a', 0, 0, 1), ('pc_y', 1, 0, 1), ('hs', 0, 0), ('pc_a', 0, 0, 0), ('pm_a', 1, 0, 1), ('pc_a', 0, 0, 1), ('pm_a', 1, 0, 0), ('hs', 0, 1), ('pc_a', 1, 0, 1), ('pc_a', 1, 0, 0), ('hs', 0, 2), ('pc_y', 1, 0, 0), ('il_y', 0, 1), ('Q_a', 1, 0), ('Q_a', 0, 0), ('hs', 0, 3), ('ma', 0, 0, 3), ('ma', 1, 0, 1), ('il_a', 0, 1), ('Q_y', 1, 0), ('ma', 1, 0, 2), ('wt_', 0, 1), ('my', 1, 0, 3), ('ea', 0, 0, 3), ('ma', 1, 0, 3), ('ea', 1, 0, 1), ('ma', 1, 0, 0), ('il_a', 1, 1), ('ea', 1, 0, 3), ('my', 1, 0, 0), ('Q_a', 0, 1), ('ma', 0, 0, 0), ('ea', 1, 0, 0), ('my', 1, 0, 2), ('Q_y', 0, 1), ('my', 1, 0, 1), ('ea', 0, 0, 0), ('ey', 1, 0, 0), ('ma', 0, 0, 2), ('Q_a', 1, 1), ('il_y', 1, 1), ('ea', 1, 0, 2), ('ma', 0, 0, 1), ('ea', 0, 0, 2), ('ma', 1, 1, 1), ('Qga', 1, 0), ('ma', 1, 1, 3), ('ea', 1, 1, 1), ('ma', 1, 1, 0), ('ey', 1, 0, 2), ('ea', 1, 1, 3), ('ma', 0, 1, 0), ('sq', 1, 1), ('Q_y', 1, 1), ('my', 0, 0, 0), ('ea', 0, 1, 0), ('my', 1, 1, 1), ('ea', 0, 0, 1), ('my', 1, 1, 0), ('ea', 1, 1, 0), ('ey', 1, 1, 1), ('my', 0, 1, 2), ('hs', 1, 2), ('ey', 1, 1, 0), ('my', 0, 1, 1), ('ey', 0, 1, 2), ('my', 1, 1, 3), ('hs', 1, 3), ('ey', 0, 1, 1), ('my', 0, 1, 0), ('ey', 0, 0, 0), ('Qga', 0, 0), ('my', 0, 0, 1), ('ey', 1, 1, 3), ('hs', 1, 1), ('my', 0, 0, 3), ('ey', 0, 1, 0), ('ey', 0, 0, 1), ('ma', 1, 1, 2), ('hs', 1, 0), ('ey', 0, 0, 3), ('my', 0, 0, 2), ('ey', 1, 0, 3), ('ma', 0, 1, 3), ('ey', 0, 0, 2), ('wt_', 0, 0), ('my', 0, 1, 3), ('ey', 1, 0, 1), ('wt_', 1, 0), ('ma', 0, 1, 1), ('il_ah', 0, 0), ('Qgy', 0, 0), ('ma', 0, 1, 2), ('Qgy', 1, 0), ('my', 1, 1, 2), ('il_ah', 1, 0), ('f', 0, 0, 2), ('f', 0, 0, 1), ('ey', 1, 1, 2), ('Q_ah', 0, 0), ('ey', 0, 1, 3), ('f', 0, 0, 3), ('Q_ah', 1, 0), ('il_ah', 0, 1), ('f', 0, 0, 0), ('ea', 0, 1, 2), ('d', 0, 0, 3), ('wt_', 1, 1), ('d', 0, 0, 2), ('Qgy', 1, 1), ('d', 0, 0, 0), ('Qgy', 0, 1), ('d', 0, 0, 1), ('v', 0, 0, 0), ('ea', 0, 1, 1), ('f', 0, 1, 2), ('v', 0, 0, 1), ('Q_ah', 0, 1), ('f', 0, 1, 1), ('v', 0, 0, 3), ('ea', 0, 1, 3), ('d', 0, 1, 2), ('v', 0, 0, 2), ('ea', 1, 1, 2), ('d', 0, 1, 1), ('il_ah', 1, 1), ('Qga', 0, 1), ('f', 0, 1, 0), ('Qga', 1, 1), ('f', 0, 1, 3), ('oi', 0, 0), ('f', 1, 0, 3), ('d', 0, 1, 3), ('v', 0, 1, 1), ('f', 1, 0, 0), ('Q_ah', 1, 1), ('f', 1, 0, 1), ('v', 0, 1, 3), ('oq', 0, 0), ('d', 1, 0, 0), ('v', 0, 1, 2), ('d', 1, 0, 1), ('v', 1, 0, 0), ('d', 1, 0, 3), ('v', 1, 0, 1), ('d', 0, 1, 0), ('v', 1, 0, 3), ('f', 1, 0, 2), ('v', 0, 1, 0), ('hf', 1, 1, 0, 0), ('oi', 0, 1), ('d', 1, 0, 2), ('hv', 1, 1, 0, 0), ('hf', 1, 1, 0, 1), ('v', 1, 0, 2), ('oq', 0, 1), ('oi', 1, 0), ('hf', 1, 1, 1, 0), ('hv', 1, 1, 0, 1), ('hi', 1, 1, 0), ('hf', 1, 1, 1, 1), ('hv', 1, 1, 1, 0), ('oq', 1, 0), ('hq', 1, 1, 0), ('hv', 1, 1, 1, 1), ('hi', 1, 1, 1), ('hq', 1, 1, 1)]
+LOADS = [('phi', 0, 0), ('phi', 1, 0), ('y', 0, 0), ('y', 1, 0), ('phi', 0, 1), ('phi', 1, 1), ('a', 0, None), ('a', 1, None), ('y', 0, 1), ('y', 1, 1)]
+ON_SCALAR = [('a', 0, 1), ('a', 1, 1), ('ah', 0, 0), ('ah', 0, 1), ('ah', 1, 1)]
+ORDER = [('il_phi', 0, 0), ('omb', 0), ('omb', 1), ('ob', 0), ('il_phi', 1, 0), ('omt',), ('ob', 1), ('pm_y', 0, 0, 0), ('oms',), ('Q_phi', 0), ('pm_y', 0, 0, 1), ('pc_y', 0, 0, 0), ('pm_y', 1, 0, 1), ('pc_y', 0, 0, 1), ('pm_y', 1, 0, 0), ('pc_y', 1, 0, 1), ('il_phi', 0, 1), ('sq', 0, 0), ('il_phi', 1, 1), ('pc_y', 1, 0, 0), ('hs', 0, 1), ('sq', 1, 0), ('pm_a', 0, 0, 0), ('Q_y', 0), ('pm_a', 0, 0, 1), ('Q_phi', 1), ('pc_a', 0, 0, 0), ('my', 0, 0, 0), ('pc_a', 0, 0, 1), ('my', 0, 0, 3), ('hs', 1, 1), ('sq', 1, 1), ('my', 1, 0, 3), ('hs', 1, 0), ('my', 1, 0, 1), ('pm_a', 1, 0, 1), ('ey', 1, 0, 3), ('hs', 0, 0), ('pm_y', 0, 1, 0), ('ey', 1, 0, 1), ('pm_a', 1, 0, 0), ('pc_a', 1, 0, 1), ('hs', 1, 3), ('pm_y', 0, 1, 1), ('pc_y', 0, 1, 0), ('pm_y', 1, 1, 0), ('pc_a', 1, 0, 0), ('hs', 1, 2), ('pm_y', 1, 1, 1), ('pc_y', 0, 1, 1), ('my', 1, 0, 0), ('pc_y', 1, 1, 0), ('Q_a', 0), ('my', 0, 0, 1), ('pc_y', 1, 1, 1), ('my', 0, 0, 2), ('ey', 1, 0, 0), ('wt', 1), ('ey', 0, 0, 3), ('ma', 0, 0, 1), ('ey', 0, 0, 2), ('ma', 1, 0, 3), ('Q_y', 1), ('il_a', 1, 1), ('ma', 0, 0, 2), ('il_ah', 1, 0), ('ma', 1, 0, 0), ('my', 1, 1, 0), ('ea', 1, 0, 3), ('my', 0, 1, 3), ('sq', 0, 1), ('ea', 0, 0, 1), ('ma', 1, 0, 2), ('ea', 1, 0, 0), ('my', 0, 1, 2), ('ea', 1, 0, 2), ('ma', 0, 0, 3), ('ey', 1, 1, 0), ('ea', 0, 0, 2), ('my', 1, 1, 2), ('ey', 0, 1, 2), ('hs', 0, 2), ('il_a', 0, 1), ('ma', 1, 0, 1), ('my', 1, 1, 1), ('ea', 0, 0, 3), ('my', 1, 1, 3), ('ea', 1, 0, 1), ('hs', 0, 3), ('my', 0, 1, 1), ('ey', 1, 1, 1), ('ma', 0, 0, 0), ('ey', 1, 1, 3), ('Q_a', 1), ('my', 0, 1, 0), ('ey', 0, 1, 1), ('ey', 0, 1, 3), ('my', 1, 0, 2), ('ea', 0, 0, 0), ('ey', 1, 1, 2), ('ma', 0, 1, 2), ('wt', 0), ('ey', 1, 0, 2), ('ma', 0, 1, 1), ('ey', 0, 0, 0), ('ma', 1, 1, 3), ('Q_ga', 0), ('ey', 0, 0, 1), ('ma', 0, 1, 3), ('il_ah', 0, 0), ('ea', 1, 1, 3), ('ma', 0, 1, 0), ('Q_gy', 0), ('ma', 1, 1, 1), ('ma', 1, 1, 0), ('ea', 0, 1, 0), ('ey', 0, 1, 0), ('ma', 1, 1, 2), ('Q_ah', 0), ('il_ah', 0, 1), ('f', 0, 0, 2), ('f', 0, 0, 1), ('ea', 1, 1, 0), ('d', 0, 0, 2), ('ea', 1, 1, 2), ('d', 0, 0, 1), ('il_ah', 1, 1), ('Q_gy', 1), ('f', 0, 0, 3), ('f', 0, 0, 0), ('ea', 0, 1, 1), ('d', 0, 0, 3), ('ea', 1, 1, 1), ('f', 0, 1, 0), ('v', 0, 0, 2), ('ea', 0, 1, 3), ('f', 0, 1, 2), ('v', 0, 0, 3), ('Q_ah', 1), ('f', 0, 1, 1), ('v', 0, 0, 1), ('d', 0, 1, 2), ('ea', 0, 1, 2), ('d', 0, 1, 1), ('v', 0, 1, 2), ('f', 0, 1, 3), ('Q_ga', 1), ('v', 0, 1, 1), ('d', 0, 1, 0), ('d', 0, 1, 3), ('v', 0, 1, 0), ('d', 0, 0, 0), ('v', 0, 1, 3), ('hf', 1, 1, 1, 0), ('v', 0, 0, 0), ('oi', 0, 1), ('f', 1, 0, 1), ('hv', 1, 1, 1, 0), ('f', 1, 0, 0), ('oi', 0, 0), ('d', 1, 0, 1), ('d', 1, 0, 0), ('v', 1, 0, 1), ('f', 1, 0, 2), ('oq', 0, 1), ('v', 1, 0, 0), ('f', 1, 0, 3), ('oq', 0, 0), ('d', 1, 0, 2), ('d', 1, 0, 3), ('v', 1, 0, 2), ('hf', 1, 1, 0, 1), ('v', 1, 0, 3), ('hf', 1, 1, 1, 1), ('oi', 1, 0), ('hv', 1, 1, 0, 1), ('hf', 1, 1, 0, 0), ('hv', 1, 1, 1, 1), ('oq', 1, 0), ('hv', 1, 1, 0, 0), ('hi', 1, 1, 1), ('hi', 1, 1, 0), ('hq', 1, 1, 1), ('hq', 1, 1, 0)]
 
 
 def tile_secondorderinfluenceustatisticmatrix_x1_kernel(tc, a, y, phi, omega, out_0, out_1, out_2):
@@ -34,8 +33,11 @@ def tile_secondorderinfluenceustatisticmatrix_x1_kernel(tc, a, y, phi, omega, ou
         psum = ctx.enter_context(tc.psum_pool(name="psum", bufs=4))
         ctx.enter_context(tc.manual_schedule())
 
-        def chunk():
-            return work.tile([P, PACK * HALF], BF16, name="chunk", tag="chunk", bufs=CHUNKS, align_bytes=64)
+        def mix_tile():
+            return work.tile([P, 2, PACK * HALF], BF16, name="mix", tag="mix", bufs=6, align_bytes=64)
+
+        def f32_tile():
+            return work.tile([P, PACK * HALF], F32, name="wide", tag="wide", bufs=5, align_bytes=64)
 
         def keep_tile(shape, dtype, name):
             return keep.tile(shape, dtype, name=name, align_bytes=64)
@@ -45,12 +47,23 @@ def tile_secondorderinfluenceustatisticmatrix_x1_kernel(tc, a, y, phi, omega, ou
         scales = {}
         group = {}
 
-        def load(key, src, g):
-            c = key[2]
-            t = chunk()[:].rearrange("p (j w) -> p j w", j=PACK)
-            rows = src[g * HALF:(g + 1) * HALF, c * HALF:(c + 1) * HALF]
-            nc.sync.dma_start(out=t, in_=rows.rearrange("(p j) w -> p j w", j=PACK))
-            raw[key] = t
+        def load(key, src):
+            name, g, c = key
+            rows = src[g * HALF:(g + 1) * HALF, :].rearrange("(p j) w -> p j w", j=PACK)
+            if (name, g) not in raw:
+                raw[name, g] = keep_tile([P, PACK, N], BF16, "raw_%s_%d" % (name, g))
+            cols = slice(0, N) if c is None else slice(c * HALF, (c + 1) * HALF)
+            nc.sync.dma_start(out=raw[name, g][:, :, cols], in_=rows[:, :, cols])
+
+        def raw_half(key):
+            name, g, c = key
+            return raw[name, g][:, :, c * HALF:(c + 1) * HALF]
+
+        def mixed(key):
+            name, g, c = key
+            if (name, c) not in group:
+                group[name, c] = mix_tile()
+            return group[name, c][:, g, :]
 
         def mix_phi(t, src):
             nc.vector.tensor_copy(
@@ -77,32 +90,35 @@ def tile_secondorderinfluenceustatisticmatrix_x1_kernel(tc, a, y, phi, omega, ou
             )
 
         def interleave(key):
-            t = chunk()
-            src = raw[key]
+            t, src = mixed(key), raw_half(key)
             if key[0] == "y":
-                mix_plain(nc.scalar.copy if key in ON_SCALAR else nc.vector.tensor_copy, t[:], src)
+                mix_plain(nc.scalar.copy if key in ON_SCALAR else nc.vector.tensor_copy, t, src)
             elif key[0] == "phi":
-                mix_phi(t[:], src)
+                mix_phi(t, src)
             elif key in ON_SCALAR:
-                mix_a_scalar(t[:], src)
+                mix_a_scalar(t, src)
             else:
-                mix_a_vector(t[:], src)
-            group[key] = t
+                mix_a_vector(t, src)
 
-        def quantize(key, src=None):
-            q = keep_tile([P, HALF], U32, "codes_%s_%d_%d" % key)
-            s = keep_tile([P, HALF], U8, "scales_%s_%d_%d" % key)
-            nc.vector.quantize_mx(out=q[:].bitcast(FP8X4), scales=s[:], in_=(group[key] if src is None else src)[:])
-            codes[key] = q
-            scales[key] = s
+        def quantize(name, c):
+            q = keep_tile([P, 2, HALF], U32, "codes_%s_%d" % (name, c))
+            s = keep_tile([P, 2, HALF], U8, "scales_%s_%d" % (name, c))
+            nc.vector.quantize_mx(
+                out=q[:].rearrange("p g w -> p (g w)").bitcast(FP8X4),
+                scales=s[:].rearrange("p g w -> p (g w)"),
+                in_=group[name, c][:].rearrange("p g w -> p (g w)"),
+            )
+            for g in range(2):
+                codes[name, g, c] = q[:, g, :]
+                scales[name, g, c] = s[:, g, :]
 
-        omega_row = keep_tile([P, N], BF16, "omega_row")
+        omega_rows = keep_tile([P, 2, N], BF16, "omega_rows")
+        omega_row, omega_p = omega_rows[:, 0, :], omega_rows[:, 1, :]
         ones = keep_tile([P, P], BF16, "ones")
         omega_b = keep_tile([P, N], BF16, "omega_b")
-        omega_p = keep_tile([P, N], BF16, "omega_p")
         omega_s = keep_tile([P, 2, PACK], F32, "omega_s")
         hneg = keep_tile([P, 2, PACK], F32, "hneg")
-        sq = [keep_tile([P, PACK, N], F32, "sq%d" % g) for g in range(2)]
+        sq = {}
 
         def bank():
             return psum.tile([P, HALF], F32, name="bank", tag="bank", bufs=8)
@@ -112,13 +128,18 @@ def tile_secondorderinfluenceustatisticmatrix_x1_kernel(tc, a, y, phi, omega, ou
         outf = {}
         og = {}
 
-        nc.vector.memset(omega_row[:], 0.0)
+        nc.vector.memset(omega_rows[:], 0.0)
         nc.vector.memset(ones[:], 1.0)
         sources = {"phi": phi, "a": a, "y": y}
         for i, key in enumerate(LOADS):
-            load(key, sources[key[0]], key[1])
-            if i == 0:
+            load(key, sources[key[0]])
+            if i == 1:
                 nc.sync.dma_start(out=omega_row[0:1, :], in_=omega.rearrange("(o k) -> o k", o=1))
+                for g in range(2):
+                    nc.sync.dma_start(
+                        out=omega_p[0:1, g * HALF:(g + 1) * HALF].rearrange("o (t b r) -> o t b r", t=PACK, b=16),
+                        in_=omega[g * HALF:(g + 1) * HALF].rearrange("(o b t r) -> o t b r", o=1, b=16, t=PACK),
+                    )
         ident = keep_tile([P, P], BF16, "ident")
         make_identity(nc, ident[:])
 
@@ -128,21 +149,13 @@ def tile_secondorderinfluenceustatisticmatrix_x1_kernel(tc, a, y, phi, omega, ou
             for i in range(2):
                 part = 2 * h + i
                 if key[0] == "y":
-                    rhs = raw[key][:, :, part * P:(part + 1) * P].rearrange("p j c -> p c j")
+                    rhs = raw_half(key)[:, :, part * P:(part + 1) * P].rearrange("p j c -> p c j")
                 else:
-                    rhs = raw[key].rearrange("p j (m t) -> p t m j", t=PACK)[:, part, :, :]
+                    rhs = raw_half(key).rearrange("p j (m t) -> p t m j", t=PACK)[:, part, :, :]
                 nc.tensor.matmul(out=b[:, i * HALF:(i + 1) * HALF].rearrange("p (c j) -> p c j", j=PACK), lhsT=ident[:], rhs=rhs, start=True, stop=True)
 
         def turn_out(key, h):
-            if key not in group:
-                group[key] = chunk()
-            nc.scalar.copy(out=group[key][:, h * 2 * HALF:(h + 1) * 2 * HALF], in_=banks["turn", key, h][:])
-
-        def omega_permute():
-            nc.vector.tensor_copy(
-                out=omega_p[:].rearrange("p (g t b r) -> p g t b r", g=2, t=PACK, b=16),
-                in_=omega_row[:].rearrange("p (g b t r) -> p g t b r", g=2, b=16, t=PACK),
-            )
+            nc.scalar.copy(out=mixed(key)[:, h * 2 * HALF:(h + 1) * 2 * HALF], in_=banks["turn", key, h][:])
 
         def omega_turn():
             spread = bank()
@@ -180,10 +193,7 @@ def tile_secondorderinfluenceustatisticmatrix_x1_kernel(tc, a, y, phi, omega, ou
 
         def s1_out(name, kg, c, block):
             cols = slice(block * P, (block + 1) * P)
-            key = ("g" + name, kg, c)
-            if key not in group:
-                group[key] = chunk()
-            dst = group[key][:].rearrange("p (n t) -> p n t", t=PACK)[:, cols, :]
+            dst = mixed(("g" + name, kg, c)).rearrange("p (n t) -> p n t", t=PACK)[:, cols, :]
             src = banks[name, kg, c, block][:].rearrange("p (t n) -> p n t", t=PACK)
             if name == "y":
                 nc.scalar.activation(out=dst, in_=src, func=COPY, scale=ROOT)
@@ -191,20 +201,22 @@ def tile_secondorderinfluenceustatisticmatrix_x1_kernel(tc, a, y, phi, omega, ou
                 w = omega_s[:, kg, :].unsqueeze(1).to_broadcast([P, P, PACK])
                 nc.vector.tensor_tensor(out=dst, in0=src, in1=w, op=MULT)
 
-        def square(g, c):
-            nc.scalar.activation(out=sq[g][:, :, c * HALF:(c + 1) * HALF], in_=raw["phi", g, c], func=SQUARE)
+        def square(g, u):
+            t = f32_tile()[:].rearrange("p (j w) -> p j w", j=2)
+            nc.scalar.activation(out=t, in_=raw["phi", g][:, 2 * u:2 * u + 2, :], func=SQUARE)
+            sq[g, u] = t
 
         def hsum(g, j):
             nc.vector.scalar_tensor_tensor(
-                out=sq[g][:, j, :], in0=sq[g][:, j, :], scalar=-1.0 / N, in1=omega_b[:],
+                out=sq[g, j // 2][:, j % 2, :], in0=sq[g, j // 2][:, j % 2, :], scalar=-1.0 / N, in1=omega_b[:],
                 op0=MULT, op1=MULT, accum_out=hneg[:, g, j:j + 1],
             )
 
-        def weigh(g, c):
-            t = chunk()[:].rearrange("p (j w) -> p j w", j=PACK)
+        def weigh(g):
+            t = keep_tile([P, PACK, N], BF16, "raw_ah_%d" % g)
             for j in range(PACK):
-                nc.vector.tensor_scalar(out=t[:, j, :], in0=raw["a", g, c][:, j, :], scalar1=hneg[:, g, j:j + 1], scalar2=None, op0=MULT)
-            raw["ah", g, c] = t
+                nc.vector.tensor_scalar(out=t[:, j, :], in0=raw["a", g][:, j, :], scalar1=hneg[:, g, j:j + 1], scalar2=None, op0=MULT)
+            raw["ah", g] = t
 
         def product(pg, c, t, diagonal):
             left, right = ("ah", "y") if diagonal else ("ga", "gy")
@@ -216,15 +228,15 @@ def tile_secondorderinfluenceustatisticmatrix_x1_kernel(tc, a, y, phi, omega, ou
                     out=banks[pg, c, t][:],
                     lhsT=codes[left, g, pg][:, ps].bitcast(FP8X4),
                     lhsT_scale=scales[left, g, pg][:, ps],
-                    rhs=codes[right, g, c][:].bitcast(FP8X4),
-                    rhs_scale=scales[right, g, c][:],
+                    rhs=codes[right, g, c].bitcast(FP8X4),
+                    rhs_scale=scales[right, g, c],
                     start=(not diagonal and g == 0),
                     stop=(diagonal and g == 1),
                 )
 
         def evacuate(pg, c, t):
             if (pg, c) not in outf:
-                outf[pg, c] = work.tile([P, PACK, HALF], F32, name="outf", tag="outf", bufs=4, align_bytes=64)
+                outf[pg, c] = f32_tile()[:].rearrange("p (t n) -> p t n", t=PACK)
             f = outf[pg, c]
             nc.scalar.activation(out=f[:, t, :], in_=banks[pg, c, t][:], func=COPY, scale=ROOT)
             stored.add((pg, c, t))
@@ -233,22 +245,28 @@ def tile_secondorderinfluenceustatisticmatrix_x1_kernel(tc, a, y, phi, omega, ou
                 dst = out_0[pg * HALF:(pg + 1) * HALF, c * HALF:(c + 1) * HALF].rearrange("(p t) m -> p t m", t=PACK)
                 nc.sync.dma_start(out=dst[:, pair, :], in_=f[:, pair, :])
 
+        scale_rows = [keep_tile([P, N], U8, "scale_rows_%d" % pg) for pg in range(2)]
+        finished = [0, 0]
+
+        def store_scales(pg, columns):
+            finished[pg] += columns
+            if finished[pg] == N:
+                rows = out_2[pg].bitcast(I32)
+                for q in range(4):
+                    nc.sync.dma_start(out=rows[4 * q:4 * q + 4, :], in_=scale_rows[pg][32 * q:32 * q + 4, :].bitcast(I32))
+
         def plane_mix(pg, c):
-            t = chunk()
-            mix_plain(nc.vector.tensor_copy, t[:], outf[pg, c][:])
+            t = work.tile([P, PACK * HALF], BF16, name="og", tag="og", bufs=2, align_bytes=64)
+            mix_plain(nc.vector.tensor_copy, t[:], outf[pg, c])
             og[pg, c] = t
 
         def plane_out(pg, c):
             key = ("o", pg, c)
-            quantize(key, og[pg, c])
+            codes[key] = keep_tile([P, HALF], U32, "codes_o_%d_%d" % (pg, c))
+            nc.vector.quantize_mx(out=codes[key][:].bitcast(FP8X4), scales=scale_rows[pg][:, c * HALF:(c + 1) * HALF], in_=og[pg, c][:])
             words = out_1[pg].rearrange("p m t -> p (m t)").bitcast(I32)
             nc.sync.dma_start(out=words[:, c * HALF:(c + 1) * HALF], in_=codes[key][:].bitcast(I32))
-            srows = out_2[pg].bitcast(I32)
-            for q in range(4):
-                nc.sync.dma_start(
-                    out=srows[4 * q:4 * q + 4, c * P:(c + 1) * P],
-                    in_=scales[key][32 * q:32 * q + 4, :].bitcast(I32),
-                )
+            store_scales(pg, HALF)
 
         def half_product(pg, c, h, u):
             b = bank()
@@ -272,38 +290,30 @@ def tile_secondorderinfluenceustatisticmatrix_x1_kernel(tc, a, y, phi, omega, ou
 
         def half_evacuate(pg, c, h, u):
             if (pg, c) not in outf:
-                outf[pg, c] = work.tile([P, PACK, HALF], F32, name="outf", tag="outf", bufs=4, align_bytes=64)
+                outf[pg, c] = f32_tile()[:].rearrange("p (t n) -> p t n", t=PACK)
             f = outf[pg, c][:, 2 * u:2 * u + 2, h * 256:(h + 1) * 256]
             nc.scalar.activation(out=f, in_=banks[pg, c, h, u][:].rearrange("p (t n) -> p t n", t=2), func=COPY, scale=ROOT)
             rows = out_0[pg * HALF:(pg + 1) * HALF, c * HALF + h * 256:c * HALF + (h + 1) * 256].rearrange("(p t) m -> p t m", t=PACK)
             nc.sync.dma_start(out=rows[:, 2 * u:2 * u + 2, :], in_=f)
 
         def half_mix(pg, c, h):
-            t = chunk()
+            t = work.tile([P, PACK * HALF], BF16, name="og", tag="og", bufs=2, align_bytes=64)
             mix_plain(nc.vector.tensor_copy, t[:, :HALF * 2], outf[pg, c][:, :, h * 256:(h + 1) * 256])
             og[pg, c, h] = t
 
         def half_out(pg, c, h):
             if ("o", pg, c) not in codes:
                 codes["o", pg, c] = keep_tile([P, HALF], U32, "codes_o_%d_%d" % (pg, c))
-                scales["o", pg, c] = keep_tile([P, HALF], U8, "scales_o_%d_%d" % (pg, c))
             cols = slice(h * 256, (h + 1) * 256)
             q = codes["o", pg, c][:, cols]
-            s = scales["o", pg, c][:, cols]
+            s = scale_rows[pg][:, c * HALF + h * 256:c * HALF + (h + 1) * 256]
             nc.vector.quantize_mx(out=q.bitcast(FP8X4), scales=s, in_=og[pg, c, h][:, :HALF * 2])
             words = out_1[pg].rearrange("p m t -> p (m t)").bitcast(I32)
             nc.sync.dma_start(out=words[:, c * HALF + h * 256:c * HALF + (h + 1) * 256], in_=q.bitcast(I32))
-            srows = out_2[pg].bitcast(I32)
-            for r in range(4):
-                nc.sync.dma_start(
-                    out=srows[4 * r:4 * r + 4, c * P + h * 64:c * P + (h + 1) * 64],
-                    in_=s[32 * r:32 * r + 4, :].bitcast(I32),
-                )
+            store_scales(pg, 256)
 
         def step(head, *digits):
-            if head == "omp":
-                omega_permute()
-            elif head == "omt":
+            if head == "omt":
                 omega_turn()
             elif head == "oms":
                 omega_scale()
@@ -315,14 +325,12 @@ def tile_secondorderinfluenceustatisticmatrix_x1_kernel(tc, a, y, phi, omega, ou
                 key = (head[3:], digits[0], digits[1])
                 interleave(key)
             elif head.startswith("Q_"):
-                quantize((head[2:], digits[0], digits[1]))
-            elif head.startswith("Qg"):
-                quantize((head[1:], digits[0], digits[1]))
+                quantize(head[2:], digits[0])
             elif head == "sq":
                 square(*digits)
             elif head == "hs":
                 hsum(*digits)
-            elif head == "wt_":
+            elif head == "wt":
                 weigh(*digits)
             elif head in ("my", "ma"):
                 s1_mm(head[1], *digits)

@@ -17,347 +17,421 @@ COPY = mybir.ActivationFunctionType.Copy
 SQUARE = mybir.ActivationFunctionType.Square
 
 P = 128
-PACK = 4
-HALF = 512
+SLOTS = 4
+HALF = P * SLOTS
+QUARTER = HALF // 2
+TILES = N // P
 ROOT = 1.0 / 32.0
-LOADS = [('phi', 0, 0), ('phi', 1, 0), ('y', 0, 0), ('y', 1, 0), ('phi', 0, 1), ('phi', 1, 1), ('a', 0, None), ('a', 1, None), ('y', 0, 1), ('y', 1, 1)]
-ON_SCALAR = [('a', 0, 1), ('a', 1, 1), ('ah', 0, 0), ('ah', 0, 1), ('ah', 1, 1)]
-ORDER = [('il_phi', 0, 0), ('omb', 0), ('omb', 1), ('ob', 0), ('il_phi', 1, 0), ('omt',), ('ob', 1), ('pm_y', 0, 0, 0), ('oms',), ('Q_phi', 0), ('pm_y', 0, 0, 1), ('pc_y', 0, 0, 0), ('pm_y', 1, 0, 1), ('pc_y', 0, 0, 1), ('pm_y', 1, 0, 0), ('pc_y', 1, 0, 1), ('il_phi', 0, 1), ('sq', 0, 0), ('il_phi', 1, 1), ('pc_y', 1, 0, 0), ('hs', 0, 1), ('sq', 1, 0), ('pm_a', 0, 0, 0), ('Q_y', 0), ('pm_a', 0, 0, 1), ('Q_phi', 1), ('pc_a', 0, 0, 0), ('my', 0, 0, 0), ('pc_a', 0, 0, 1), ('my', 0, 0, 3), ('hs', 1, 1), ('sq', 1, 1), ('my', 1, 0, 3), ('hs', 1, 0), ('my', 1, 0, 1), ('pm_a', 1, 0, 1), ('ey', 1, 0, 3), ('hs', 0, 0), ('pm_y', 0, 1, 0), ('ey', 1, 0, 1), ('pm_a', 1, 0, 0), ('pc_a', 1, 0, 1), ('hs', 1, 3), ('pm_y', 0, 1, 1), ('pc_y', 0, 1, 0), ('pm_y', 1, 1, 0), ('pc_a', 1, 0, 0), ('hs', 1, 2), ('pm_y', 1, 1, 1), ('pc_y', 0, 1, 1), ('my', 1, 0, 0), ('pc_y', 1, 1, 0), ('Q_a', 0), ('my', 0, 0, 1), ('pc_y', 1, 1, 1), ('my', 0, 0, 2), ('ey', 1, 0, 0), ('wt', 1), ('ey', 0, 0, 3), ('ma', 0, 0, 1), ('ey', 0, 0, 2), ('ma', 1, 0, 3), ('Q_y', 1), ('il_a', 1, 1), ('ma', 0, 0, 2), ('il_ah', 1, 0), ('ma', 1, 0, 0), ('my', 1, 1, 0), ('ea', 1, 0, 3), ('my', 0, 1, 3), ('sq', 0, 1), ('ea', 0, 0, 1), ('ma', 1, 0, 2), ('ea', 1, 0, 0), ('my', 0, 1, 2), ('ea', 1, 0, 2), ('ma', 0, 0, 3), ('ey', 1, 1, 0), ('ea', 0, 0, 2), ('my', 1, 1, 2), ('ey', 0, 1, 2), ('hs', 0, 2), ('il_a', 0, 1), ('ma', 1, 0, 1), ('my', 1, 1, 1), ('ea', 0, 0, 3), ('my', 1, 1, 3), ('ea', 1, 0, 1), ('hs', 0, 3), ('my', 0, 1, 1), ('ey', 1, 1, 1), ('ma', 0, 0, 0), ('ey', 1, 1, 3), ('Q_a', 1), ('my', 0, 1, 0), ('ey', 0, 1, 1), ('ey', 0, 1, 3), ('my', 1, 0, 2), ('ea', 0, 0, 0), ('ey', 1, 1, 2), ('ma', 0, 1, 2), ('wt', 0), ('ey', 1, 0, 2), ('ma', 0, 1, 1), ('ey', 0, 0, 0), ('ma', 1, 1, 3), ('Q_ga', 0), ('ey', 0, 0, 1), ('ma', 0, 1, 3), ('il_ah', 0, 0), ('ea', 1, 1, 3), ('ma', 0, 1, 0), ('Q_gy', 0), ('ma', 1, 1, 1), ('ma', 1, 1, 0), ('ea', 0, 1, 0), ('ey', 0, 1, 0), ('ma', 1, 1, 2), ('Q_ah', 0), ('il_ah', 0, 1), ('f', 0, 0, 2), ('f', 0, 0, 1), ('ea', 1, 1, 0), ('d', 0, 0, 2), ('ea', 1, 1, 2), ('d', 0, 0, 1), ('il_ah', 1, 1), ('Q_gy', 1), ('f', 0, 0, 3), ('f', 0, 0, 0), ('ea', 0, 1, 1), ('d', 0, 0, 3), ('ea', 1, 1, 1), ('f', 0, 1, 0), ('v', 0, 0, 2), ('ea', 0, 1, 3), ('f', 0, 1, 2), ('v', 0, 0, 3), ('Q_ah', 1), ('f', 0, 1, 1), ('v', 0, 0, 1), ('d', 0, 1, 2), ('ea', 0, 1, 2), ('d', 0, 1, 1), ('v', 0, 1, 2), ('f', 0, 1, 3), ('Q_ga', 1), ('v', 0, 1, 1), ('d', 0, 1, 0), ('d', 0, 1, 3), ('v', 0, 1, 0), ('d', 0, 0, 0), ('v', 0, 1, 3), ('hf', 1, 1, 1, 0), ('v', 0, 0, 0), ('oi', 0, 1), ('f', 1, 0, 1), ('hv', 1, 1, 1, 0), ('f', 1, 0, 0), ('oi', 0, 0), ('d', 1, 0, 1), ('d', 1, 0, 0), ('v', 1, 0, 1), ('f', 1, 0, 2), ('oq', 0, 1), ('v', 1, 0, 0), ('f', 1, 0, 3), ('oq', 0, 0), ('d', 1, 0, 2), ('d', 1, 0, 3), ('v', 1, 0, 2), ('hf', 1, 1, 0, 1), ('v', 1, 0, 3), ('hf', 1, 1, 1, 1), ('oi', 1, 0), ('hv', 1, 1, 0, 1), ('hf', 1, 1, 0, 0), ('hv', 1, 1, 1, 1), ('oq', 1, 0), ('hv', 1, 1, 0, 0), ('hi', 1, 1, 1), ('hi', 1, 1, 0), ('hq', 1, 1, 1), ('hq', 1, 1, 0)]
+BANKS = 8
 
 
 def tile_secondorderinfluenceustatisticmatrix_x1_kernel(tc, a, y, phi, omega, out_0, out_1, out_2):
     nc = tc.nc
     with ExitStack() as ctx:
         keep = ctx.enter_context(tc.tile_pool(name="keep", bufs=1))
-        work = ctx.enter_context(tc.tile_pool(name="work", bufs=3))
-        psum = ctx.enter_context(tc.psum_pool(name="psum", bufs=4))
+        work = ctx.enter_context(tc.tile_pool(name="work", bufs=2))
+        psum = ctx.enter_context(tc.psum_pool(name="psum", bufs=BANKS))
         ctx.enter_context(tc.manual_schedule())
-
-        def mix_tile():
-            return work.tile([P, 2, PACK * HALF], BF16, name="mix", tag="mix", bufs=6, align_bytes=64)
-
-        def f32_tile():
-            return work.tile([P, PACK * HALF], F32, name="wide", tag="wide", bufs=5, align_bytes=64)
 
         def keep_tile(shape, dtype, name):
             return keep.tile(shape, dtype, name=name, align_bytes=64)
 
+        def bank(dtype=F32):
+            columns = HALF if dtype == F32 else 2 * HALF
+            return psum.tile([P, columns], dtype, name="bank", tag="bank", bufs=BANKS)
+
+        def wide_tile():
+            return work.tile([P, SLOTS * HALF], F32, name="wide", tag="wide", bufs=5, align_bytes=64)
+
         raw = {}
+        weighted = {}
+        mixed = {}
         codes = {}
         scales = {}
-        group = {}
+        banks = {}
+        squares = {}
+        result = {}
+        ordered = {}
 
-        def load(key, src):
-            name, g, c = key
-            rows = src[g * HALF:(g + 1) * HALF, :].rearrange("(p j) w -> p j w", j=PACK)
+        source = {"phi": phi, "y": y, "a": a}
+
+        def load(name, g, half):
             if (name, g) not in raw:
-                raw[name, g] = keep_tile([P, PACK, N], BF16, "raw_%s_%d" % (name, g))
-            cols = slice(0, N) if c is None else slice(c * HALF, (c + 1) * HALF)
-            nc.sync.dma_start(out=raw[name, g][:, :, cols], in_=rows[:, :, cols])
+                raw[name, g] = keep_tile([P, 2, SLOTS, HALF], BF16, "raw_%s_%d" % (name, g))
+            block = source[name][g * HALF:(g + 1) * HALF, half * HALF:(half + 1) * HALF]
+            nc.sync.dma_start(out=raw[name, g][:, half, :, :], in_=block.rearrange("(p j) w -> p j w", j=SLOTS))
 
-        def raw_half(key):
-            name, g, c = key
-            return raw[name, g][:, :, c * HALF:(c + 1) * HALF]
+        def mixed_rows(name, g, half):
+            if (name, half) not in mixed:
+                mixed[name, half] = work.tile([P, 2, SLOTS * HALF], BF16, name="mixed", tag="mixed", bufs=6, align_bytes=64)
+            return mixed[name, half][:, g, :]
 
-        def mixed(key):
-            name, g, c = key
-            if (name, c) not in group:
-                group[name, c] = mix_tile()
-            return group[name, c][:, g, :]
+        def raw_half(name, g, half):
+            if name == "ah":
+                return weighted[g][:, :, half, :]
+            return raw[name, g][:, half, :, :]
 
-        def mix_phi(t, src):
-            nc.vector.tensor_copy(
-                out=t.rearrange("p (t b r j) -> p t b r j", t=PACK, b=16, j=PACK),
-                in_=src.rearrange("p j (b t r) -> p t b r j", b=16, t=PACK),
-            )
-
-        def mix_a_vector(t, src):
-            nc.vector.tensor_copy(
-                out=t.rearrange("p (t m n j) -> p m t n j", t=PACK, n=2, j=PACK),
-                in_=src.rearrange("p j (m n t) -> p m t n j", n=2, t=PACK),
-            )
-
-        def mix_a_scalar(t, src):
-            nc.scalar.copy(
-                out=t.rearrange("p (t m j) -> p m j t", t=PACK, j=PACK),
-                in_=src.rearrange("p j (m t) -> p m j t", t=PACK),
-            )
-
-        def mix_plain(copy, t, src):
+        def mix_plain(copy, dst, src):
             copy(
-                out=t.rearrange("p (c i j) -> p c j i", i=4, j=PACK),
+                out=dst.rearrange("p (c i j) -> p c j i", i=4, j=SLOTS),
                 in_=src.rearrange("p j (c i) -> p c j i", i=4),
             )
 
-        def interleave(key):
-            t, src = mixed(key), raw_half(key)
-            if key[0] == "y":
-                mix_plain(nc.scalar.copy if key in ON_SCALAR else nc.vector.tensor_copy, t, src)
-            elif key[0] == "phi":
-                mix_phi(t, src)
-            elif key in ON_SCALAR:
-                mix_a_scalar(t, src)
-            else:
-                mix_a_vector(t, src)
+        def mix_slots_vector(name, g, half):
+            nc.vector.tensor_copy(
+                out=mixed_rows(name, g, half).rearrange("p (t u v j) -> p u t v j", t=SLOTS, v=2, j=SLOTS),
+                in_=raw_half(name, g, half).rearrange("p j (u v t) -> p u t v j", v=2, t=SLOTS),
+            )
 
-        def quantize(name, c):
-            q = keep_tile([P, 2, HALF], U32, "codes_%s_%d" % (name, c))
-            s = keep_tile([P, 2, HALF], U8, "scales_%s_%d" % (name, c))
+        def mix_slots_scalar(name, g, half):
+            nc.scalar.copy(
+                out=mixed_rows(name, g, half).rearrange("p (t m j) -> p m j t", t=SLOTS, j=SLOTS),
+                in_=raw_half(name, g, half).rearrange("p j (m t) -> p m j t", t=SLOTS),
+            )
+
+        def mix_y_vector(g, half):
+            mix_plain(nc.vector.tensor_copy, mixed_rows("y", g, half), raw_half("y", g, half))
+
+        def mix_y_scalar(g, half):
+            mix_plain(nc.scalar.copy, mixed_rows("y", g, half), raw_half("y", g, half))
+
+        def quantize(name, half):
+            q = keep_tile([P, 2, HALF], U32, "codes_%s_%d" % (name, half))
+            s = keep_tile([P, 2, HALF], U8, "scales_%s_%d" % (name, half))
             nc.vector.quantize_mx(
                 out=q[:].rearrange("p g w -> p (g w)").bitcast(FP8X4),
                 scales=s[:].rearrange("p g w -> p (g w)"),
-                in_=group[name, c][:].rearrange("p g w -> p (g w)"),
+                in_=mixed[name, half][:].rearrange("p g w -> p (g w)"),
             )
             for g in range(2):
-                codes[name, g, c] = q[:, g, :]
-                scales[name, g, c] = s[:, g, :]
+                codes[name, g, half] = q[:, g, :]
+                scales[name, g, half] = s[:, g, :]
 
-        omega_rows = keep_tile([P, 2, N], BF16, "omega_rows")
-        omega_row, omega_p = omega_rows[:, 0, :], omega_rows[:, 1, :]
+        omega_row = keep_tile([P, N], BF16, "omega_row")
         ones = keep_tile([P, P], BF16, "ones")
-        omega_b = keep_tile([P, N], BF16, "omega_b")
-        omega_s = keep_tile([P, 2, PACK], F32, "omega_s")
-        hneg = keep_tile([P, 2, PACK], F32, "hneg")
-        sq = {}
+        omega_wide = keep_tile([P, N], BF16, "omega_wide")
+        omega_slots = keep_tile([P, 2, SLOTS], F32, "omega_slots")
+        omega_tiles = keep_tile([P, TILES], F32, "omega_tiles")
+        identity = keep_tile([P, P], BF16, "identity")
+        identity_f32 = keep_tile([P, P], F32, "identity_f32")
 
-        def bank():
-            return psum.tile([P, HALF], F32, name="bank", tag="bank", bufs=8)
+        def load_omega():
+            nc.sync.dma_start(out=omega_row[0:1, :], in_=omega.rearrange("(o k) -> o k", o=1))
 
-        banks = {}
-        stored = set()
-        outf = {}
-        og = {}
+        def spread_omega():
+            for h in range(2):
+                banks["omega", h] = bank()
+                columns = slice(h * HALF, (h + 1) * HALF)
+                nc.tensor.matmul(out=banks["omega", h][:], lhsT=ones[:], rhs=omega_row[:, columns], start=True, stop=True)
+            for h in range(2):
+                nc.scalar.copy(out=omega_wide[:, h * HALF:(h + 1) * HALF], in_=banks["omega", h][:])
 
-        nc.vector.memset(omega_rows[:], 0.0)
-        nc.vector.memset(ones[:], 1.0)
-        sources = {"phi": phi, "a": a, "y": y}
-        for i, key in enumerate(LOADS):
-            load(key, sources[key[0]])
-            if i == 1:
-                nc.sync.dma_start(out=omega_row[0:1, :], in_=omega.rearrange("(o k) -> o k", o=1))
-                for g in range(2):
-                    nc.sync.dma_start(
-                        out=omega_p[0:1, g * HALF:(g + 1) * HALF].rearrange("o (t b r) -> o t b r", t=PACK, b=16),
-                        in_=omega[g * HALF:(g + 1) * HALF].rearrange("(o b t r) -> o t b r", o=1, b=16, t=PACK),
-                    )
-        ident = keep_tile([P, P], BF16, "ident")
-        make_identity(nc, ident[:])
-
-        def turn(key, h):
-            b = psum.tile([P, 2 * HALF], BF16, name="bank", tag="bank", bufs=8)
-            banks["turn", key, h] = b
-            for i in range(2):
-                part = 2 * h + i
-                if key[0] == "y":
-                    rhs = raw_half(key)[:, :, part * P:(part + 1) * P].rearrange("p j c -> p c j")
-                else:
-                    rhs = raw_half(key).rearrange("p j (m t) -> p t m j", t=PACK)[:, part, :, :]
-                nc.tensor.matmul(out=b[:, i * HALF:(i + 1) * HALF].rearrange("p (c j) -> p c j", j=PACK), lhsT=ident[:], rhs=rhs, start=True, stop=True)
-
-        def turn_out(key, h):
-            nc.scalar.copy(out=mixed(key)[:, h * 2 * HALF:(h + 1) * 2 * HALF], in_=banks["turn", key, h][:])
-
-        def omega_turn():
-            spread = bank()
-            banks["spread"] = spread
-            for i in range(2 * PACK):
-                nc.tensor.matmul(out=spread[:, i:i + 1], lhsT=omega_p[:, i * P:(i + 1) * P], rhs=ones[:, 0:1], start=True, stop=True)
-
-        def omega_scale():
-            nc.scalar.activation(out=omega_s[:], in_=banks["spread"][:, :2 * PACK].rearrange("p (g t) -> p g t", g=2), func=COPY, scale=ROOT)
-
-        def omega_mm(c):
-            banks["omega", c] = bank()
-            nc.tensor.matmul(out=banks["omega", c][:], lhsT=ones[:], rhs=omega_row[:, c * HALF:(c + 1) * HALF], start=True, stop=True)
-
-        def omega_out(c):
-            nc.scalar.copy(out=omega_b[:, c * HALF:(c + 1) * HALF], in_=banks["omega", c][:])
-
-        def s1_mm(name, kg, c, block):
+        def turn_omega():
             b = bank()
-            banks[name, kg, c, block] = b
-            cols = slice(block * P, (block + 1) * P)
-            b4 = b[:].rearrange("p (t n) -> p t n", t=PACK)
-            for t in range(PACK):
-                ks = slice(t * P, (t + 1) * P)
-                for g in range(2):
-                    nc.tensor.matmul_mx(
-                        out=b4[:, t, :],
-                        lhsT=codes["phi", g, kg][:, ks].bitcast(FP8X4),
-                        lhsT_scale=scales["phi", g, kg][:, ks],
-                        rhs=codes[name, g, c][:, cols].bitcast(FP8X4),
-                        rhs_scale=scales[name, g, c][:, cols],
-                        start=(g == 0),
-                        stop=(g == 1),
-                    )
+            banks["omega columns"] = b
+            slots = omega_row[:].rearrange("p (h m t) -> p h t m", h=2, t=SLOTS)
+            for i in range(TILES):
+                column = b[:, i:i + 1]
+                nc.tensor.matmul(out=column, lhsT=slots[:, i // SLOTS, i % SLOTS, :], rhs=ones[:, 0:1], start=True, stop=True)
+            for i in range(TILES):
+                column = b[:, TILES + i:TILES + i + 1]
+                nc.tensor.matmul(out=column, lhsT=omega_row[:, i * P:(i + 1) * P], rhs=ones[:, 0:1], start=True, stop=True)
 
-        def s1_out(name, kg, c, block):
-            cols = slice(block * P, (block + 1) * P)
-            dst = mixed(("g" + name, kg, c)).rearrange("p (n t) -> p n t", t=PACK)[:, cols, :]
-            src = banks[name, kg, c, block][:].rearrange("p (t n) -> p n t", t=PACK)
-            if name == "y":
-                nc.scalar.activation(out=dst, in_=src, func=COPY, scale=ROOT)
-            else:
-                w = omega_s[:, kg, :].unsqueeze(1).to_broadcast([P, P, PACK])
-                nc.vector.tensor_tensor(out=dst, in0=src, in1=w, op=MULT)
+        def keep_omega():
+            b = banks["omega columns"]
+            nc.scalar.activation(
+                out=omega_slots[:], in_=b[:, :TILES].rearrange("p (h t) -> p h t", h=2), func=COPY, scale=ROOT,
+            )
+            nc.scalar.copy(out=omega_tiles[:], in_=b[:, TILES:2 * TILES])
 
-        def square(g, u):
-            t = f32_tile()[:].rearrange("p (j w) -> p j w", j=2)
-            nc.scalar.activation(out=t, in_=raw["phi", g][:, 2 * u:2 * u + 2, :], func=SQUARE)
-            sq[g, u] = t
+        weights = keep_tile([P, 2, SLOTS], F32, "weights")
 
-        def hsum(g, j):
+        def square_tile(g, j):
+            if (g, j // 2) not in squares:
+                squares[g, j // 2] = wide_tile()[:].rearrange("p (j w) -> p j w", j=2)
+            return squares[g, j // 2][:, j % 2, :]
+
+        def square(pair):
+            square_tile(0, 2 * pair)
+            nc.scalar.activation(
+                out=squares[0, pair].rearrange("p j (h w) -> p h j w", h=2),
+                in_=raw["phi", 0][:, :, 2 * pair:2 * pair + 2, :], func=SQUARE,
+            )
+
+        def weighted_sum(j):
             nc.vector.scalar_tensor_tensor(
-                out=sq[g, j // 2][:, j % 2, :], in0=sq[g, j // 2][:, j % 2, :], scalar=-1.0 / N, in1=omega_b[:],
-                op0=MULT, op1=MULT, accum_out=hneg[:, g, j:j + 1],
+                out=square_tile(0, j), in0=square_tile(0, j), scalar=-1.0 / N, in1=omega_wide[:],
+                op0=MULT, op1=MULT, accum_out=weights[:, 0, j:j + 1],
+            )
+
+        def turn_phi(j):
+            b = bank(BF16)
+            banks["turned", j] = b
+            for i in range(TILES):
+                half, first = divmod(i * P, HALF)
+                block = raw["phi", 1][:, half, j, first:first + P]
+                nc.tensor.transpose(out=b[:, i * P:(i + 1) * P], in_=block, identity=identity[:])
+
+        def square_turned(j):
+            nc.scalar.activation(out=square_tile(1, j), in_=banks["turned", j][:], func=SQUARE)
+
+        def sum_turned(j):
+            b = bank()
+            banks["sums", j] = b
+            for i in range(TILES):
+                nc.tensor.matmul(
+                    out=b[:, :P], lhsT=omega_tiles[:, i:i + 1].to_broadcast([P, P]),
+                    rhs=square_tile(1, j)[:, i * P:(i + 1) * P], start=(i == 0), stop=(i == TILES - 1),
+                )
+
+        def pick_diagonal(j):
+            picked = work.tile([P, P], F32, name="picked", tag="picked", bufs=2, align_bytes=64)
+            nc.vector.scalar_tensor_tensor(
+                out=picked[:], in0=banks["sums", j][:, :P], scalar=-1.0 / N, in1=identity_f32[:],
+                op0=MULT, op1=MULT, accum_out=weights[:, 1, j:j + 1],
             )
 
         def weigh(g):
-            t = keep_tile([P, PACK, N], BF16, "raw_ah_%d" % g)
-            for j in range(PACK):
-                nc.vector.tensor_scalar(out=t[:, j, :], in0=raw["a", g][:, j, :], scalar1=hneg[:, g, j:j + 1], scalar2=None, op0=MULT)
-            raw["ah", g] = t
-
-        def product(pg, c, t, diagonal):
-            left, right = ("ah", "y") if diagonal else ("ga", "gy")
-            if not diagonal:
-                banks[pg, c, t] = bank()
-            ps = slice(t * P, (t + 1) * P)
-            for g in range(2):
-                nc.tensor.matmul_mx(
-                    out=banks[pg, c, t][:],
-                    lhsT=codes[left, g, pg][:, ps].bitcast(FP8X4),
-                    lhsT_scale=scales[left, g, pg][:, ps],
-                    rhs=codes[right, g, c].bitcast(FP8X4),
-                    rhs_scale=scales[right, g, c],
-                    start=(not diagonal and g == 0),
-                    stop=(diagonal and g == 1),
+            weighted[g] = keep_tile([P, SLOTS, 2, HALF], BF16, "weighted_%d" % g)
+            for j in range(SLOTS):
+                nc.vector.tensor_scalar(
+                    out=weighted[g][:, j, :, :], in0=raw["a", g][:, :, j, :], scalar1=weights[:, g, j:j + 1], scalar2=None, op0=MULT,
                 )
 
-        def evacuate(pg, c, t):
-            if (pg, c) not in outf:
-                outf[pg, c] = f32_tile()[:].rearrange("p (t n) -> p t n", t=PACK)
-            f = outf[pg, c]
-            nc.scalar.activation(out=f[:, t, :], in_=banks[pg, c, t][:], func=COPY, scale=ROOT)
-            stored.add((pg, c, t))
-            if (pg, c, t ^ 1) in stored:
-                pair = slice(t - t % 2, t - t % 2 + 2)
-                dst = out_0[pg * HALF:(pg + 1) * HALF, c * HALF:(c + 1) * HALF].rearrange("(p t) m -> p t m", t=PACK)
-                nc.sync.dma_start(out=dst[:, pair, :], in_=f[:, pair, :])
-
-        scale_rows = [keep_tile([P, N], U8, "scale_rows_%d" % pg) for pg in range(2)]
-        finished = [0, 0]
-
-        def store_scales(pg, columns):
-            finished[pg] += columns
-            if finished[pg] == N:
-                rows = out_2[pg].bitcast(I32)
-                for q in range(4):
-                    nc.sync.dma_start(out=rows[4 * q:4 * q + 4, :], in_=scale_rows[pg][32 * q:32 * q + 4, :].bitcast(I32))
-
-        def plane_mix(pg, c):
-            t = work.tile([P, PACK * HALF], BF16, name="og", tag="og", bufs=2, align_bytes=64)
-            mix_plain(nc.vector.tensor_copy, t[:], outf[pg, c])
-            og[pg, c] = t
-
-        def plane_out(pg, c):
-            key = ("o", pg, c)
-            codes[key] = keep_tile([P, HALF], U32, "codes_o_%d_%d" % (pg, c))
-            nc.vector.quantize_mx(out=codes[key][:].bitcast(FP8X4), scales=scale_rows[pg][:, c * HALF:(c + 1) * HALF], in_=og[pg, c][:])
-            words = out_1[pg].rearrange("p m t -> p (m t)").bitcast(I32)
-            nc.sync.dma_start(out=words[:, c * HALF:(c + 1) * HALF], in_=codes[key][:].bitcast(I32))
-            store_scales(pg, HALF)
-
-        def half_product(pg, c, h, u):
-            b = bank()
-            banks[pg, c, h, u] = b
-            cols = slice(h * 256, (h + 1) * 256)
-            for i in range(2):
-                t = 2 * u + i
-                ps = slice(t * P, (t + 1) * P)
-                for diagonal in (False, True):
-                    left, right = ("ah", "y") if diagonal else ("ga", "gy")
+        def stage1(name, h, half):
+            for block in range(SLOTS):
+                b = bank()
+                banks[name, h, half, block] = b
+                columns = slice(block * P, (block + 1) * P)
+                for t in range(SLOTS):
+                    slot = slice(t * P, (t + 1) * P)
                     for g in range(2):
                         nc.tensor.matmul_mx(
-                            out=b[:, i * 256:(i + 1) * 256],
-                            lhsT=codes[left, g, pg][:, ps].bitcast(FP8X4),
-                            lhsT_scale=scales[left, g, pg][:, ps],
-                            rhs=codes[right, g, c][:, cols].bitcast(FP8X4),
-                            rhs_scale=scales[right, g, c][:, cols],
-                            start=(not diagonal and g == 0),
-                            stop=(diagonal and g == 1),
+                            out=b[:, slot],
+                            lhsT=codes["phi", g, h][:, slot].bitcast(FP8X4),
+                            lhsT_scale=scales["phi", g, h][:, slot],
+                            rhs=codes[name, g, half][:, columns].bitcast(FP8X4),
+                            rhs_scale=scales[name, g, half][:, columns],
+                            start=(g == 0),
+                            stop=(g == 1),
                         )
 
-        def half_evacuate(pg, c, h, u):
-            if (pg, c) not in outf:
-                outf[pg, c] = f32_tile()[:].rearrange("p (t n) -> p t n", t=PACK)
-            f = outf[pg, c][:, 2 * u:2 * u + 2, h * 256:(h + 1) * 256]
-            nc.scalar.activation(out=f, in_=banks[pg, c, h, u][:].rearrange("p (t n) -> p t n", t=2), func=COPY, scale=ROOT)
-            rows = out_0[pg * HALF:(pg + 1) * HALF, c * HALF + h * 256:c * HALF + (h + 1) * 256].rearrange("(p t) m -> p t m", t=PACK)
-            nc.sync.dma_start(out=rows[:, 2 * u:2 * u + 2, :], in_=f)
+        def stage1_out(name, h, half, block):
+            columns = slice(block * P, (block + 1) * P)
+            dst = mixed_rows("g" + name, h, half).rearrange("p (n t) -> p n t", t=SLOTS)[:, columns, :]
+            return dst, banks[name, h, half, block][:].rearrange("p (t n) -> p n t", t=SLOTS)
 
-        def half_mix(pg, c, h):
-            t = work.tile([P, PACK * HALF], BF16, name="og", tag="og", bufs=2, align_bytes=64)
-            mix_plain(nc.vector.tensor_copy, t[:, :HALF * 2], outf[pg, c][:, :, h * 256:(h + 1) * 256])
-            og[pg, c, h] = t
+        def g1_out(h, half):
+            factor = omega_slots[:, h, :].unsqueeze(1).to_broadcast([P, P, SLOTS])
+            for block in range(SLOTS):
+                dst, src = stage1_out("a", h, half, block)
+                nc.vector.tensor_tensor(out=dst, in0=src, in1=factor, op=MULT)
 
-        def half_out(pg, c, h):
-            if ("o", pg, c) not in codes:
-                codes["o", pg, c] = keep_tile([P, HALF], U32, "codes_o_%d_%d" % (pg, c))
-            cols = slice(h * 256, (h + 1) * 256)
-            q = codes["o", pg, c][:, cols]
-            s = scale_rows[pg][:, c * HALF + h * 256:c * HALF + (h + 1) * 256]
-            nc.vector.quantize_mx(out=q.bitcast(FP8X4), scales=s, in_=og[pg, c, h][:, :HALF * 2])
-            words = out_1[pg].rearrange("p m t -> p (m t)").bitcast(I32)
-            nc.sync.dma_start(out=words[:, c * HALF + h * 256:c * HALF + (h + 1) * 256], in_=q.bitcast(I32))
-            store_scales(pg, 256)
+        def g2_out(h, half):
+            for block in range(SLOTS):
+                dst, src = stage1_out("y", h, half, block)
+                nc.scalar.activation(out=dst, in_=src, func=COPY, scale=ROOT)
 
-        def step(head, *digits):
-            if head == "omt":
-                omega_turn()
-            elif head == "oms":
-                omega_scale()
-            elif head == "omb":
-                omega_mm(*digits)
-            elif head == "ob":
-                omega_out(*digits)
-            elif head.startswith("il_"):
-                key = (head[3:], digits[0], digits[1])
-                interleave(key)
-            elif head.startswith("Q_"):
-                quantize(head[2:], digits[0])
-            elif head == "sq":
-                square(*digits)
-            elif head == "hs":
-                hsum(*digits)
-            elif head == "wt":
-                weigh(*digits)
-            elif head in ("my", "ma"):
-                s1_mm(head[1], *digits)
-            elif head in ("ey", "ea"):
-                s1_out(head[1], *digits)
-            elif head in ("f", "d"):
-                product(digits[0], digits[1], digits[2], head == "d")
-            elif head == "v":
-                evacuate(*digits)
-            elif head.startswith("pm_"):
-                turn((head[3:], digits[0], digits[1]), digits[2])
-            elif head.startswith("pc_"):
-                turn_out((head[3:], digits[0], digits[1]), digits[2])
-            elif head == "hf":
-                half_product(*digits)
-            elif head == "hv":
-                half_evacuate(*digits)
-            elif head == "hi":
-                half_mix(*digits)
-            elif head == "hq":
-                half_out(*digits)
-            elif head == "oi":
-                plane_mix(*digits)
-            elif head == "oq":
-                plane_out(*digits)
-            else:
-                raise ValueError(head)
+        def passes(out, rh, t, ch, columns, left, right, first, last):
+            slot = slice(t * P, (t + 1) * P)
+            for g in range(2):
+                nc.tensor.matmul_mx(
+                    out=out,
+                    lhsT=codes[left, g, rh][:, slot].bitcast(FP8X4),
+                    lhsT_scale=scales[left, g, rh][:, slot],
+                    rhs=codes[right, g, ch][:, columns].bitcast(FP8X4),
+                    rhs_scale=scales[right, g, ch][:, columns],
+                    start=(first and g == 0),
+                    stop=(last and g == 1),
+                )
 
-        for entry in ORDER:
-            step(*entry)
+        def full_passes(rh, ch):
+            for t in range(SLOTS):
+                banks["out", rh, ch, t] = bank()
+                passes(banks["out", rh, ch, t][:], rh, t, ch, slice(0, HALF), "ga", "gy", True, False)
+
+        def diagonal_passes(rh, ch):
+            for t in range(SLOTS):
+                passes(banks["out", rh, ch, t][:], rh, t, ch, slice(0, HALF), "ah", "y", False, True)
+
+        def out_rows(rh, ch):
+            rows = out_0[rh * HALF:(rh + 1) * HALF, ch * HALF:(ch + 1) * HALF]
+            return rows.rearrange("(p t) m -> p t m", t=SLOTS)
+
+        def out_of_banks(rh, ch):
+            r = wide_tile()[:].rearrange("p (t n) -> p t n", t=SLOTS)
+            result[rh, ch] = r
+            for t in range(SLOTS):
+                nc.scalar.activation(out=r[:, t, :], in_=banks["out", rh, ch, t][:], func=COPY, scale=ROOT)
+                if t % 2:
+                    nc.sync.dma_start(out=out_rows(rh, ch)[:, t - 1:t + 1, :], in_=r[:, t - 1:t + 1, :])
+
+        def both_passes(rh, ch, part):
+            columns = slice(part * QUARTER, (part + 1) * QUARTER)
+            for u in range(2):
+                b = bank()
+                banks["part", part, u] = b
+                for v in range(2):
+                    dst = b[:, v * QUARTER:(v + 1) * QUARTER]
+                    passes(dst, rh, 2 * u + v, ch, columns, "ga", "gy", True, False)
+                    passes(dst, rh, 2 * u + v, ch, columns, "ah", "y", False, True)
+
+        def part_out_of_banks(rh, ch, part):
+            columns = slice(part * QUARTER, (part + 1) * QUARTER)
+            if part == 0:
+                result["parts"] = wide_tile()
+            part_rows = result["parts"][:, part * SLOTS * QUARTER:(part + 1) * SLOTS * QUARTER]
+            result["part", part] = part_rows.rearrange("p (t n) -> p t n", t=SLOTS)
+            for u in range(2):
+                dst = result["part", part][:, 2 * u:2 * u + 2, :]
+                src = banks["part", part, u][:].rearrange("p (t n) -> p t n", t=2)
+                nc.scalar.activation(out=dst, in_=src, func=COPY, scale=ROOT)
+                nc.sync.dma_start(out=out_rows(rh, ch)[:, 2 * u:2 * u + 2, columns], in_=dst)
+
+        out_scales = [keep_tile([P, N], U8, "out_scales_%d" % rh) for rh in range(2)]
+
+        def mix_rows(key, rows, width):
+            o = work.tile([P, SLOTS * HALF], BF16, name="ordered", tag="ordered", bufs=2, align_bytes=64)
+            ordered[key] = o[:, :SLOTS * width]
+            mix_plain(nc.vector.tensor_copy, ordered[key], rows)
+
+        def mix_result(rh, ch):
+            mix_rows((rh, ch), result[rh, ch], HALF)
+
+        def mix_part(part):
+            mix_rows(("part", part), result["part", part], QUARTER)
+
+        def quantize_rows(key, rh, first, width):
+            q = keep_tile([P, width], U32, "out_codes_%d_%d" % (rh, first))
+            columns = slice(first, first + width)
+            nc.vector.quantize_mx(
+                out=q[:].bitcast(FP8X4), scales=out_scales[rh][:, columns], in_=ordered[key],
+            )
+            words = out_1[rh].rearrange("p m t -> p (m t)").bitcast(I32)
+            nc.sync.dma_start(out=words[:, columns], in_=q[:].bitcast(I32))
+
+        def quantize_result(rh, ch):
+            quantize_rows((rh, ch), rh, ch * HALF, HALF)
+
+        def quantize_part(rh, ch, part):
+            quantize_rows(("part", part), rh, ch * HALF + part * QUARTER, QUARTER)
+
+        def store_scales(rh):
+            rows = out_2[rh].bitcast(I32)
+            for r in range(4):
+                nc.sync.dma_start(
+                    out=rows[4 * r:4 * r + 4, :], in_=out_scales[rh][32 * r:32 * r + 4, :].bitcast(I32),
+                )
+
+        nc.vector.memset(omega_row[:], 0.0)
+        nc.vector.memset(ones[:], 1.0)
+        make_identity(nc, identity[:])
+        make_identity(nc, identity_f32[:])
+        load("phi", 1, 0)
+        load("phi", 1, 1)
+        load_omega()
+        load("phi", 0, 0)
+        load("phi", 0, 1)
+        for half in range(2):
+            for name in ("y", "a"):
+                for g in range(2):
+                    load(name, g, half)
+
+        mix_slots_vector("phi", 1, 0)
+        spread_omega()
+        mix_slots_vector("phi", 1, 1)
+        turn_phi(0)
+        turn_phi(1)
+        square_turned(0)
+        mix_slots_vector("phi", 0, 0)
+        turn_phi(2)
+        turn_omega()
+        square_turned(1)
+        mix_slots_vector("phi", 0, 1)
+        turn_phi(3)
+        keep_omega()
+        square(0)
+        sum_turned(0)
+        mix_y_vector(0, 0)
+        quantize("phi", 1)
+        square_turned(2)
+        sum_turned(1)
+        mix_y_vector(1, 0)
+        square(1)
+        sum_turned(2)
+        pick_diagonal(0)
+        quantize("y", 0)
+        square_turned(3)
+        weighted_sum(0)
+        mix_slots_scalar("a", 0, 0)
+        stage1("y", 1, 0)
+        mix_slots_vector("a", 1, 0)
+        weighted_sum(1)
+        g2_out(1, 0)
+        sum_turned(3)
+        pick_diagonal(1)
+        quantize("a", 0)
+        weighted_sum(2)
+
+        mix_y_scalar(0, 1)
+        stage1("a", 1, 0)
+        pick_diagonal(2)
+        quantize("phi", 0)
+        mix_y_scalar(1, 1)
+        g1_out(1, 0)
+        stage1("y", 0, 0)
+        g2_out(0, 0)
+        pick_diagonal(3)
+        quantize("y", 1)
+        stage1("a", 0, 0)
+        weighted_sum(3)
+        mix_slots_scalar("a", 1, 1)
+        g1_out(0, 0)
+        stage1("y", 1, 1)
+        mix_slots_scalar("a", 0, 1)
+        weigh(1)
+        stage1("y", 0, 1)
+        quantize("ga", 0)
+        g2_out(1, 1)
+        quantize("a", 1)
+        quantize("gy", 0)
+        g2_out(0, 1)
+        stage1("a", 1, 1)
+        weigh(0)
+        mix_slots_vector("ah", 1, 0)
+        mix_slots_scalar("ah", 0, 0)
+
+        full_passes(0, 0)
+        g1_out(1, 1)
+        mix_slots_scalar("ah", 1, 1)
+        stage1("a", 0, 1)
+        quantize("ah", 0)
+        mix_slots_scalar("ah", 0, 1)
+        quantize("gy", 1)
+        diagonal_passes(0, 0)
+        g1_out(0, 1)
+        out_of_banks(0, 0)
+        full_passes(0, 1)
+        quantize("ga", 1)
+        diagonal_passes(0, 1)
+        quantize("ah", 1)
+        out_of_banks(0, 1)
+        mix_result(0, 0)
+        full_passes(1, 0)
+        quantize_result(0, 0)
+        mix_result(0, 1)
+        diagonal_passes(1, 0)
+        out_of_banks(1, 0)
+        both_passes(1, 1, 0)
+        mix_result(1, 0)
+        part_out_of_banks(1, 1, 0)
+        both_passes(1, 1, 1)
+        quantize_result(0, 1)
+        store_scales(0)
+        mix_part(0)
+        part_out_of_banks(1, 1, 1)
+        quantize_part(1, 1, 0)
+        quantize_result(1, 0)
+        mix_part(1)
+        quantize_part(1, 1, 1)
+        store_scales(1)

from contextlib import ExitStack

import concourse.mybir as mybir
from concourse.masks import make_identity

N = 1024
FLOPS = 4 * 2 * N * N * N

F32 = mybir.dt.float32
BF16 = mybir.dt.bfloat16
U32 = mybir.dt.uint32
I32 = mybir.dt.int32
U8 = mybir.dt.uint8
FP8X4 = mybir.dt.float8_e4m3fn_x4
MULT = mybir.AluOpType.mult
COPY = mybir.ActivationFunctionType.Copy
SQUARE = mybir.ActivationFunctionType.Square

P = 128
SLOTS = 4
HALF = P * SLOTS
QUARTER = HALF // 2
TILES = N // P
ROOT = 1.0 / 32.0
BANKS = 8


def tile_secondorderinfluenceustatisticmatrix_x1_kernel(tc, a, y, phi, omega, out_0, out_1, out_2):
    nc = tc.nc
    with ExitStack() as ctx:
        keep = ctx.enter_context(tc.tile_pool(name="keep", bufs=1))
        work = ctx.enter_context(tc.tile_pool(name="work", bufs=2))
        psum = ctx.enter_context(tc.psum_pool(name="psum", bufs=BANKS))
        ctx.enter_context(tc.manual_schedule())

        def keep_tile(shape, dtype, name):
            return keep.tile(shape, dtype, name=name, align_bytes=64)

        def bank(dtype=F32):
            columns = HALF if dtype == F32 else 2 * HALF
            return psum.tile([P, columns], dtype, name="bank", tag="bank", bufs=BANKS)

        def wide_tile():
            return work.tile([P, SLOTS * HALF], F32, name="wide", tag="wide", bufs=5, align_bytes=64)

        raw = {}
        weighted = {}
        mixed = {}
        codes = {}
        scales = {}
        banks = {}
        squares = {}
        result = {}
        ordered = {}

        source = {"phi": phi, "y": y, "a": a}

        def load(name, g, half):
            if (name, g) not in raw:
                raw[name, g] = keep_tile([P, 2, SLOTS, HALF], BF16, "raw_%s_%d" % (name, g))
            block = source[name][g * HALF:(g + 1) * HALF, half * HALF:(half + 1) * HALF]
            nc.sync.dma_start(out=raw[name, g][:, half, :, :], in_=block.rearrange("(p j) w -> p j w", j=SLOTS))

        def mixed_rows(name, g, half):
            if (name, half) not in mixed:
                mixed[name, half] = work.tile([P, 2, SLOTS * HALF], BF16, name="mixed", tag="mixed", bufs=6, align_bytes=64)
            return mixed[name, half][:, g, :]

        def raw_half(name, g, half):
            if name == "ah":
                return weighted[g][:, :, half, :]
            return raw[name, g][:, half, :, :]

        def mix_plain(copy, dst, src):
            copy(
                out=dst.rearrange("p (c i j) -> p c j i", i=4, j=SLOTS),
                in_=src.rearrange("p j (c i) -> p c j i", i=4),
            )

        def mix_slots_vector(name, g, half):
            nc.vector.tensor_copy(
                out=mixed_rows(name, g, half).rearrange("p (t u v j) -> p u t v j", t=SLOTS, v=2, j=SLOTS),
                in_=raw_half(name, g, half).rearrange("p j (u v t) -> p u t v j", v=2, t=SLOTS),
            )

        def mix_slots_scalar(name, g, half):
            nc.scalar.copy(
                out=mixed_rows(name, g, half).rearrange("p (t m j) -> p m j t", t=SLOTS, j=SLOTS),
                in_=raw_half(name, g, half).rearrange("p j (m t) -> p m j t", t=SLOTS),
            )

        def mix_y_vector(g, half):
            mix_plain(nc.vector.tensor_copy, mixed_rows("y", g, half), raw_half("y", g, half))

        def mix_y_scalar(g, half):
            mix_plain(nc.scalar.copy, mixed_rows("y", g, half), raw_half("y", g, half))

        def quantize(name, half):
            q = keep_tile([P, 2, HALF], U32, "codes_%s_%d" % (name, half))
            s = keep_tile([P, 2, HALF], U8, "scales_%s_%d" % (name, half))
            nc.vector.quantize_mx(
                out=q[:].rearrange("p g w -> p (g w)").bitcast(FP8X4),
                scales=s[:].rearrange("p g w -> p (g w)"),
                in_=mixed[name, half][:].rearrange("p g w -> p (g w)"),
            )
            for g in range(2):
                codes[name, g, half] = q[:, g, :]
                scales[name, g, half] = s[:, g, :]

        omega_row = keep_tile([P, N], BF16, "omega_row")
        ones = keep_tile([P, P], BF16, "ones")
        omega_wide = keep_tile([P, N], BF16, "omega_wide")
        omega_slots = keep_tile([P, 2, SLOTS], F32, "omega_slots")
        omega_tiles = keep_tile([P, TILES], F32, "omega_tiles")
        identity = keep_tile([P, P], BF16, "identity")
        identity_f32 = keep_tile([P, P], F32, "identity_f32")

        def load_omega():
            nc.sync.dma_start(out=omega_row[0:1, :], in_=omega.rearrange("(o k) -> o k", o=1))

        def spread_omega():
            for h in range(2):
                banks["omega", h] = bank()
                columns = slice(h * HALF, (h + 1) * HALF)
                nc.tensor.matmul(out=banks["omega", h][:], lhsT=ones[:], rhs=omega_row[:, columns], start=True, stop=True)
            for h in range(2):
                nc.scalar.copy(out=omega_wide[:, h * HALF:(h + 1) * HALF], in_=banks["omega", h][:])

        def turn_omega():
            b = bank()
            banks["omega columns"] = b
            slots = omega_row[:].rearrange("p (h m t) -> p h t m", h=2, t=SLOTS)
            for i in range(TILES):
                column = b[:, i:i + 1]
                nc.tensor.matmul(out=column, lhsT=slots[:, i // SLOTS, i % SLOTS, :], rhs=ones[:, 0:1], start=True, stop=True)
            for i in range(TILES):
                column = b[:, TILES + i:TILES + i + 1]
                nc.tensor.matmul(out=column, lhsT=omega_row[:, i * P:(i + 1) * P], rhs=ones[:, 0:1], start=True, stop=True)

        def keep_omega():
            b = banks["omega columns"]
            nc.scalar.activation(
                out=omega_slots[:], in_=b[:, :TILES].rearrange("p (h t) -> p h t", h=2), func=COPY, scale=ROOT,
            )
            nc.scalar.copy(out=omega_tiles[:], in_=b[:, TILES:2 * TILES])

        weights = keep_tile([P, 2, SLOTS], F32, "weights")

        def square_tile(g, j):
            if (g, j // 2) not in squares:
                squares[g, j // 2] = wide_tile()[:].rearrange("p (j w) -> p j w", j=2)
            return squares[g, j // 2][:, j % 2, :]

        def square(pair):
            square_tile(0, 2 * pair)
            nc.scalar.activation(
                out=squares[0, pair].rearrange("p j (h w) -> p h j w", h=2),
                in_=raw["phi", 0][:, :, 2 * pair:2 * pair + 2, :], func=SQUARE,
            )

        def weighted_sum(j):
            nc.vector.scalar_tensor_tensor(
                out=square_tile(0, j), in0=square_tile(0, j), scalar=-1.0 / N, in1=omega_wide[:],
                op0=MULT, op1=MULT, accum_out=weights[:, 0, j:j + 1],
            )

        def turn_phi(j):
            b = bank(BF16)
            banks["turned", j] = b
            for i in range(TILES):
                half, first = divmod(i * P, HALF)
                block = raw["phi", 1][:, half, j, first:first + P]
                nc.tensor.transpose(out=b[:, i * P:(i + 1) * P], in_=block, identity=identity[:])

        def square_turned(j):
            nc.scalar.activation(out=square_tile(1, j), in_=banks["turned", j][:], func=SQUARE)

        def sum_turned(j):
            b = bank()
            banks["sums", j] = b
            for i in range(TILES):
                nc.tensor.matmul(
                    out=b[:, :P], lhsT=omega_tiles[:, i:i + 1].to_broadcast([P, P]),
                    rhs=square_tile(1, j)[:, i * P:(i + 1) * P], start=(i == 0), stop=(i == TILES - 1),
                )

        def pick_diagonal(j):
            picked = work.tile([P, P], F32, name="picked", tag="picked", bufs=2, align_bytes=64)
            nc.vector.scalar_tensor_tensor(
                out=picked[:], in0=banks["sums", j][:, :P], scalar=-1.0 / N, in1=identity_f32[:],
                op0=MULT, op1=MULT, accum_out=weights[:, 1, j:j + 1],
            )

        def weigh(g):
            weighted[g] = keep_tile([P, SLOTS, 2, HALF], BF16, "weighted_%d" % g)
            for j in range(SLOTS):
                nc.vector.tensor_scalar(
                    out=weighted[g][:, j, :, :], in0=raw["a", g][:, :, j, :], scalar1=weights[:, g, j:j + 1], scalar2=None, op0=MULT,
                )

        def stage1(name, h, half):
            for block in range(SLOTS):
                b = bank()
                banks[name, h, half, block] = b
                columns = slice(block * P, (block + 1) * P)
                for t in range(SLOTS):
                    slot = slice(t * P, (t + 1) * P)
                    for g in range(2):
                        nc.tensor.matmul_mx(
                            out=b[:, slot],
                            lhsT=codes["phi", g, h][:, slot].bitcast(FP8X4),
                            lhsT_scale=scales["phi", g, h][:, slot],
                            rhs=codes[name, g, half][:, columns].bitcast(FP8X4),
                            rhs_scale=scales[name, g, half][:, columns],
                            start=(g == 0),
                            stop=(g == 1),
                        )

        def stage1_out(name, h, half, block):
            columns = slice(block * P, (block + 1) * P)
            dst = mixed_rows("g" + name, h, half).rearrange("p (n t) -> p n t", t=SLOTS)[:, columns, :]
            return dst, banks[name, h, half, block][:].rearrange("p (t n) -> p n t", t=SLOTS)

        def g1_out(h, half):
            factor = omega_slots[:, h, :].unsqueeze(1).to_broadcast([P, P, SLOTS])
            for block in range(SLOTS):
                dst, src = stage1_out("a", h, half, block)
                nc.vector.tensor_tensor(out=dst, in0=src, in1=factor, op=MULT)

        def g2_out(h, half):
            for block in range(SLOTS):
                dst, src = stage1_out("y", h, half, block)
                nc.scalar.activation(out=dst, in_=src, func=COPY, scale=ROOT)

        def passes(out, rh, t, ch, columns, left, right, first, last):
            slot = slice(t * P, (t + 1) * P)
            for g in range(2):
                nc.tensor.matmul_mx(
                    out=out,
                    lhsT=codes[left, g, rh][:, slot].bitcast(FP8X4),
                    lhsT_scale=scales[left, g, rh][:, slot],
                    rhs=codes[right, g, ch][:, columns].bitcast(FP8X4),
                    rhs_scale=scales[right, g, ch][:, columns],
                    start=(first and g == 0),
                    stop=(last and g == 1),
                )

        def full_passes(rh, ch):
            for t in range(SLOTS):
                banks["out", rh, ch, t] = bank()
                passes(banks["out", rh, ch, t][:], rh, t, ch, slice(0, HALF), "ga", "gy", True, False)

        def diagonal_passes(rh, ch):
            for t in range(SLOTS):
                passes(banks["out", rh, ch, t][:], rh, t, ch, slice(0, HALF), "ah", "y", False, True)

        def out_rows(rh, ch):
            rows = out_0[rh * HALF:(rh + 1) * HALF, ch * HALF:(ch + 1) * HALF]
            return rows.rearrange("(p t) m -> p t m", t=SLOTS)

        def out_of_banks(rh, ch):
            r = wide_tile()[:].rearrange("p (t n) -> p t n", t=SLOTS)
            result[rh, ch] = r
            for t in range(SLOTS):
                nc.scalar.activation(out=r[:, t, :], in_=banks["out", rh, ch, t][:], func=COPY, scale=ROOT)
                if t % 2:
                    nc.sync.dma_start(out=out_rows(rh, ch)[:, t - 1:t + 1, :], in_=r[:, t - 1:t + 1, :])

        def both_passes(rh, ch, part):
            columns = slice(part * QUARTER, (part + 1) * QUARTER)
            for u in range(2):
                b = bank()
                banks["part", part, u] = b
                for v in range(2):
                    dst = b[:, v * QUARTER:(v + 1) * QUARTER]
                    passes(dst, rh, 2 * u + v, ch, columns, "ga", "gy", True, False)
                    passes(dst, rh, 2 * u + v, ch, columns, "ah", "y", False, True)

        def part_out_of_banks(rh, ch, part):
            columns = slice(part * QUARTER, (part + 1) * QUARTER)
            if part == 0:
                result["parts"] = wide_tile()
            part_rows = result["parts"][:, part * SLOTS * QUARTER:(part + 1) * SLOTS * QUARTER]
            result["part", part] = part_rows.rearrange("p (t n) -> p t n", t=SLOTS)
            for u in range(2):
                dst = result["part", part][:, 2 * u:2 * u + 2, :]
                src = banks["part", part, u][:].rearrange("p (t n) -> p t n", t=2)
                nc.scalar.activation(out=dst, in_=src, func=COPY, scale=ROOT)
                nc.sync.dma_start(out=out_rows(rh, ch)[:, 2 * u:2 * u + 2, columns], in_=dst)

        out_scales = [keep_tile([P, N], U8, "out_scales_%d" % rh) for rh in range(2)]

        def mix_rows(key, rows, width):
            o = work.tile([P, SLOTS * HALF], BF16, name="ordered", tag="ordered", bufs=2, align_bytes=64)
            ordered[key] = o[:, :SLOTS * width]
            mix_plain(nc.vector.tensor_copy, ordered[key], rows)

        def mix_result(rh, ch):
            mix_rows((rh, ch), result[rh, ch], HALF)

        def mix_part(part):
            mix_rows(("part", part), result["part", part], QUARTER)

        def quantize_rows(key, rh, first, width):
            q = keep_tile([P, width], U32, "out_codes_%d_%d" % (rh, first))
            columns = slice(first, first + width)
            nc.vector.quantize_mx(
                out=q[:].bitcast(FP8X4), scales=out_scales[rh][:, columns], in_=ordered[key],
            )
            words = out_1[rh].rearrange("p m t -> p (m t)").bitcast(I32)
            nc.sync.dma_start(out=words[:, columns], in_=q[:].bitcast(I32))

        def quantize_result(rh, ch):
            quantize_rows((rh, ch), rh, ch * HALF, HALF)

        def quantize_part(rh, ch, part):
            quantize_rows(("part", part), rh, ch * HALF + part * QUARTER, QUARTER)

        def store_scales(rh):
            rows = out_2[rh].bitcast(I32)
            for r in range(4):
                nc.sync.dma_start(
                    out=rows[4 * r:4 * r + 4, :], in_=out_scales[rh][32 * r:32 * r + 4, :].bitcast(I32),
                )

        nc.vector.memset(omega_row[:], 0.0)
        nc.vector.memset(ones[:], 1.0)
        make_identity(nc, identity[:])
        make_identity(nc, identity_f32[:])
        load("phi", 1, 0)
        load("phi", 1, 1)
        load_omega()
        load("phi", 0, 0)
        load("phi", 0, 1)
        for half in range(2):
            for name in ("y", "a"):
                for g in range(2):
                    load(name, g, half)

        mix_slots_vector("phi", 1, 0)
        spread_omega()
        mix_slots_vector("phi", 1, 1)
        turn_phi(0)
        turn_phi(1)
        square_turned(0)
        mix_slots_vector("phi", 0, 0)
        turn_phi(2)
        turn_omega()
        square_turned(1)
        mix_slots_vector("phi", 0, 1)
        turn_phi(3)
        keep_omega()
        square(0)
        sum_turned(0)
        mix_y_vector(0, 0)
        quantize("phi", 1)
        square_turned(2)
        sum_turned(1)
        mix_y_vector(1, 0)
        square(1)
        sum_turned(2)
        pick_diagonal(0)
        quantize("y", 0)
        square_turned(3)
        weighted_sum(0)
        mix_slots_scalar("a", 0, 0)
        stage1("y", 1, 0)
        mix_slots_vector("a", 1, 0)
        weighted_sum(1)
        g2_out(1, 0)
        sum_turned(3)
        pick_diagonal(1)
        quantize("a", 0)
        weighted_sum(2)

        mix_y_scalar(0, 1)
        stage1("a", 1, 0)
        pick_diagonal(2)
        quantize("phi", 0)
        mix_y_scalar(1, 1)
        g1_out(1, 0)
        stage1("y", 0, 0)
        g2_out(0, 0)
        pick_diagonal(3)
        quantize("y", 1)
        stage1("a", 0, 0)
        weighted_sum(3)
        mix_slots_scalar("a", 1, 1)
        g1_out(0, 0)
        stage1("y", 1, 1)
        mix_slots_scalar("a", 0, 1)
        weigh(1)
        stage1("y", 0, 1)
        quantize("ga", 0)
        g2_out(1, 1)
        quantize("a", 1)
        quantize("gy", 0)
        g2_out(0, 1)
        stage1("a", 1, 1)
        weigh(0)
        mix_slots_vector("ah", 1, 0)
        mix_slots_scalar("ah", 0, 0)

        full_passes(0, 0)
        g1_out(1, 1)
        mix_slots_scalar("ah", 1, 1)
        stage1("a", 0, 1)
        quantize("ah", 0)
        mix_slots_scalar("ah", 0, 1)
        quantize("gy", 1)
        diagonal_passes(0, 0)
        g1_out(0, 1)
        out_of_banks(0, 0)
        full_passes(0, 1)
        quantize("ga", 1)
        diagonal_passes(0, 1)
        quantize("ah", 1)
        out_of_banks(0, 1)
        mix_result(0, 0)
        full_passes(1, 0)
        quantize_result(0, 0)
        mix_result(0, 1)
        diagonal_passes(1, 0)
        out_of_banks(1, 0)
        both_passes(1, 1, 0)
        mix_result(1, 0)
        part_out_of_banks(1, 1, 0)
        both_passes(1, 1, 1)
        quantize_result(0, 1)
        store_scales(0)
        mix_part(0)
        part_out_of_banks(1, 1, 1)
        quantize_part(1, 1, 0)
        quantize_result(1, 0)
        mix_part(1)
        quantize_part(1, 1, 1)
        store_scales(1)
